import numpy as np, ml_dtypes
CORES = [3,11,19,27,35,43,51,59]
N = 8
BF = ml_dtypes.bfloat16
def gentries(a):
    return np.ascontiguousarray(a.reshape(8, 16, -1).transpose(0, 2, 1)).reshape(8, -1)
def gtable(e):
    e = np.asarray(e); return np.ascontiguousarray(e.reshape(8, -1, 16).transpose(0, 2, 1)).reshape(128, -1).astype(np.int32)
V, M, J, T, S, H = 4096, 48, 5, 2, 5, 11
L = J * M
def base(rng):
    c = np.arange(V)
    lv = rng.integers(0, 64, (N, 8, 1, V)); lv[:, 1::2] = (c * 127) // V
    x = lv + rng.integers(0, 128, (N, 8, 16, V))
    k = rng.integers(0, V, (N, 8, 16, V)); k[:, 1::2] = (c + rng.integers(-(V // 32), V // 8, (N, 4, 16, V))) & (V - 1)
    z = rng.integers(20, 200, (N, 8, 1, T, M)) + rng.integers(0, 56, (N, 8, 16, T, M))
    return x, k, z, rng.integers(0, V, (N, 8, T, J, M))
def pack(x, k, z, v):
    return {"x0": np.ascontiguousarray(x.reshape(N, 128, V)).astype(np.float32).astype(BF), "k0": np.ascontiguousarray(k.reshape(N, 128, V)).astype(np.int32),
            "z0": np.ascontiguousarray(z.reshape(N, 128, T * M)).astype(np.float32).astype(BF), "v0": np.stack([gtable(a.reshape(8, -1)) for a in v])}
def setup_inputs(rng):
    return pack(*base(rng))
def setup_inputs_spread(rng):
    x = (np.exp2(8 * rng.random((N, 8, 1, V))) * rng.random((N, 8, 16, V))).astype(np.int64)
    z = (np.exp2(8 * rng.random((N, 8, 1, T, M))) * rng.random((N, 8, 16, T, M))).astype(np.int64)
    return pack(x, (V * rng.random((N, 8, 16, V)) ** 2).astype(np.int64), z, (V * rng.random((N, 8, T, J, M)) ** 3).astype(np.int64))
def setup_inputs_ends(rng):
    def tips(hi, *shape):
        return hi * rng.integers(0, 2, shape)
    h = rng.random((N, 8, 1, V)); x = np.where(h < 0.25, 255, np.where(h < 0.5, 0, tips(255, N, 8, 16, V)))
    k = np.where(rng.random((N, 8, 16, V)) < 0.8, tips(V - 1, N, 8, 16, V), rng.integers(8, V - 1, (N, 8, 16, V)))
    h = rng.random((N, 8, 1, T, M)); z = np.where(h < 0.3, 0, np.where(h < 0.6, 255, 255 * (rng.random((N, 8, 16, T, M)) < 0.25)))
    v = np.where(rng.random((N, 8, T, J, M)) < 0.7, tips(V - 1, N, 8, T, J, M), rng.integers(8, V - 1, (N, 8, T, J, M)))
    even = ((np.arange(N)[:, None] + np.arange(8)[None, :] + N) & 1 == 0)[:, :, None]
    x[..., V - 1] = np.where(even, 255, x[..., V - 1]); x[..., 0] = np.where(even, x[..., 0], 255)
    i = np.arange(16); nl = H + 1 - (H & 1)
    z[:, :, :, 0, M - 1] = 0; z[:, :, :, 0, M - 2] = np.where(i < H, 254, 255); z[:, :, :, 0, M - 3] = np.where(i < nl, 254, 255)
    v[:, :, 0, :, M - 2:] = V - 1; k[:, :, 0, V - 1] = V - 1
    x[..., 2579] = 255; k[:, :, 0, 2] = 2579; k[:, :, 0, 3] = V - 1; v[:, :, 0, 0, M - 3] = 2; v[:, :, 0, 1, M - 3] = 3
    x[..., 7] = 255 - (np.argsort(rng.random((N, 8, 16)), axis=2) == 0).astype(np.int64)
    k[:, :, :15, 6] = 7; k[:, :, 15, 6] = np.where(even[:, :, 0], V - 1, 0); z[:, :, :, 0, M - 5] = 0; v[:, :, 0, :, M - 5] = 6
    z[:, :, :, 0, M - 4] = z[:, :, :, 0, M - 3]; x[..., 911] = 255; x[..., 4093] = 255
    k[:, :, 0, 4] = 911; k[:, :, 0, 5] = 4093; v[:, :, 0, 0, M - 4] = 4; v[:, :, 0, 1, M - 4] = 5
    return pack(x, k, z, v)
def setup_inputs_corners(rng):
    x, k, z, v = base(rng); o = rng.permutation(8); c = np.arange(V)
    x[:, o[0], 8:] = 0
    x[:, o[1]] = rng.integers(1, 101, (N, 16, V)); z[:, o[1]] = 0; h = int(rng.integers(0, N))
    x[np.array([h, (h - J) % N]), o[1]] = rng.integers(200, 256, (2, 16, V)); z[:, o[1], :, 1:] = rng.integers(100, 150, (N, 16, T - 1, M))
    k[:, o[2]] = c
    k[:, o[3]] = (c + 1) & (V - 1); x[:, o[3]] = np.where(c % (S + 1) == 0, rng.integers(200, 256, (N, 16, V)), 0); z[:, o[3]] = rng.integers(100, 151, (N, 16, T, M))
    d = rng.integers(1, S + 2, (N, T, J, M))
    d[:, 0, :, 0] = S + 1; d[:, 0, :, 1] = S; d[:, 0, 0, 2] = S; d[:, 0, 1:, 2] = S + 1; d[:, 0, :-1, 3] = S; d[:, 0, -1, 3] = 1
    v[:, o[3]] = (rng.integers(0, V // (S + 1) - 1, (N, T, J, M)) + 1) * (S + 1) - d; v[:, o[3], 0, 0, 4] = V - 1
    x[:, o[4]] = 255 * (np.argsort(rng.random((N, 16, V)), axis=1) < H - 1 + (c & 3)); k[:, o[4]] = (rng.integers(0, V, (N, 16, V)) & (V - 4)) | (c & 3); z[:, o[4]] = 100
    k[:, o[5]] = (V - 1) * rng.integers(0, 2, (N, 16, V)); v[:, o[5]] = (V - 1) * rng.integers(0, 2, (N, T, J, M))
    h = rng.integers(0, 5, (N, 16, V))
    k[:, o[6]] = np.where(h == 0, 0, np.where(h == 1, V - 1, np.where(h == 2, c, np.where(h == 3, (c + 1) & (V - 1), (c - 1) & (V - 1)))))
    v[:, o[6]] = rng.choice(np.array([0, 1, V - 2, V - 1]), (N, T, J, M))
    v[:, o[7]] = rng.integers(0, V, (T, 1, 1))
    return pack(x, k, z, v)
def setup_inputs_ties(rng):
    x, k, z, v = base(rng)
    x = rng.integers(100, 103, x.shape); z = rng.integers(100, 102, z.shape); z[..., ::8] = 102
    for q in range(N):
        for g in range(0, 8, 2):
            few = rng.permutation(V)[:64]; few[0] = V - 1; k[q, g] = few[rng.integers(0, 64, (16, V))]
    k[:, ::3, 8:] = k[:, ::3, :8]
    k[:, 7, 14:, 1::2] = V - 1; x[:, 7, :, V - 1] = 103
    return pack(x, k, z, v)
def setup_inputs_meets(rng):
    x, k, z, v = base(rng)
    for q in range(N):
        for g in range(8):
            n = 8 + 16 * g; few = rng.permutation(V)[:n]; few[0] = 0; few[1] = V - 1
            k[q, g][:, few] = few[rng.integers(0, n, (16, n))]
            for j in range(1, J + 1): v[(q - j) % N, g, :, j - 1] = few[rng.integers(0, n, (T, M))]
    return pack(x, k, z, v)
def check_inputs(d):
    bad = []
    for k, lo, hi in (("x0", 0, 255), ("k0", 0, V - 1), ("z0", 0, 255), ("v0", 0, V - 1)):
        a = np.asarray(d[k]).astype(np.float64)
        if not (np.min(a) >= lo and np.max(a) <= hi): bad.append("range of " + k)
        elif np.any(a != np.floor(a)): bad.append("whole numbers of " + k)
    return bad
def to_hosts(a):
    return np.stack([np.concatenate([a[(q - j) % N, :, j - 1] for j in range(1, J + 1)], axis=1) for q in range(N)])
def to_owners(a):
    return np.stack([np.stack([a[(r + j) % N, :, (j - 1) * M:j * M] for j in range(1, J + 1)], axis=1) for r in range(N)])
def lowest(n, on):
    a = np.flatnonzero(on)
    return a[np.unique(n[a], return_index=True)[1]]
def reference(x0, k0, z0, v0):
    X = x0.astype(np.float32).astype(np.int64).reshape(N, 8, 16, V); K = k0.astype(np.int64).reshape(N, 8, 16, V)
    Z = z0.astype(np.float32).astype(np.int64).reshape(N, 8, 16, T, M); start = np.stack([gentries(a) for a in v0]).astype(np.int64).reshape(N, 8, T, J, M)
    odd = np.zeros(N, np.int64)
    for t in range(T):
        v = to_hosts(start[:, :, t])
        z = np.stack([np.concatenate([Z[(q - j) % N, :, :, t] for j in range(1, J + 1)], axis=2) for q in range(N)])
        b = np.full((N, 8, L), S + 1, np.int64); zb = np.zeros((N, 8, 16, L), np.int64); wb = np.zeros((N, 8, L), np.int64)
        logv, logk = [], []
        for s in range(1, S + 1):
            kv = np.take_along_axis(K, v[:, :, None, :], 3)
            ix = kv.transpose(0, 1, 3, 2).reshape(N, 8, L * 16)
            xk = np.take_along_axis(X, ix[:, :, None, :], 3).reshape(N, 8, 16, L, 16)
            score = np.add.reduce(np.maximum(xk - z[..., None], 0), axis=2)
            k = np.argmax(score, axis=-1)
            w = np.take_along_axis(kv, k[:, :, None, :], 2)[:, :, 0]
            xw = np.take_along_axis(X, w[:, :, None, :], 3)
            bid = np.add.reduce((xw > z).astype(np.int64), axis=2) >= H + odd[:, None, None]
            z = (z + xw) >> 1
            now = bid & (b > S)
            b = np.where(now, s, b); wb = np.where(now, w, wb); zb = np.where(now[:, :, None, :], z, zb)
            logv.append(v); logk.append(k); v = w
        u = (wb * np.add.reduce(zb, axis=2)) & (V - 1)
        bo = to_owners(b); win = np.argmin(bo, axis=2); first = np.min(bo, axis=2)
        uo = np.take_along_axis(to_owners(u), win[:, :, None, :], 2)
        every = np.zeros((N, 8, J, M), np.int64)
        end = to_hosts(every + first[:, :, None, :]); uw = to_hosts(every + uo)
        won = to_hosts(win[:, :, None, :] == np.arange(J)[None, None, :, None]) & (end <= S); lost = ~won & (end <= S)
        for q in range(N):
            for g in range(8):
                a = lowest(wb[q, g], won[q, g]); n = wb[q, g, a]
                X[q, g][:, n] = (X[q, g][:, n] + zb[q, g][:, a]) >> 1
                for s in range(S, 0, -1):
                    a = lowest(logv[s - 1][q, g], lost[q, g] & (end[q, g] >= s))
                    n = logv[s - 1][q, g, a]; i = logk[s - 1][q, g, a]; c = K[q, g, i, n]
                    K[q, g, i, n] = (((uw[q, g, a] * c) >> 5) + c + s) & (V - 1)
        odd = np.add.reduce(won.reshape(N, -1).astype(np.int64), axis=1) & 1
    f8 = np.arange(1, 9)[None, None, :, None]
    return {"yx": np.add.reduce(X.reshape(N, 128, 8, V // 8) * f8, axis=2).astype(np.float32), "yk": np.add.reduce(K.reshape(N, 128, 8, V // 8) * f8, axis=2).astype(np.float32)}

@@ -1,0 +1,622 @@
+import math
+from concourse.bass import DstId, RemoteDMATransfer
+from concourse.mybir import AluOpType, AxisListType, ActivationFunctionType
+
+OP = AluOpType
+AF = ActivationFunctionType
+NB, LN = 2, (128, 112)
+CHUNKS = (((0, 32), (32, 64), (64, 96), (96, 128)), ((0, 32), (32, 64), (64, 96), (96, 112)))
+ON_S = ((0, 3),)
+EQ_S = (1, 0, 5)
+BIG = 1048576.0
+MAG = 8388608.0
+MSG = 126
+
+SCRATCH = {}
+VIEW = {}
+PACK = {"float32": "pkf", "int32": "pki", "bfloat16": "pkb", "float16": "pkh", "uint16": "pku"}
+OWN = ("zl", "vl", "snd", "land", "YX", "YK", "PS0", "PS1", "RV0", "RV1")
+
+
+def _sb(name, cols, dtype, where="sbuf"):
+    if where == "sbuf" and cols <= 512 and name not in OWN:
+        pk = PACK[dtype]
+        at = SCRATCH[pk][1][1] if pk in SCRATCH else 0
+        SCRATCH[pk] = (where, [128, at + (cols + 31) // 32 * 32], dtype)
+        VIEW[name] = (pk, at, cols)
+    else:
+        SCRATCH[name] = (where, [128, cols], dtype)
+        VIEW[name] = (name, 0, cols)
+
+
+for _n, _c, _d in (
+        ("Xt", 4352, "bfloat16"), ("Kt", 4352, "int32"), ("zl", 96, "bfloat16"), ("vl", 30, "int32"),
+        ("snd", MSG, "float16"), ("land", 5 * MSG, "float16"), ("ones", 2048, "bfloat16"), ("E", 2048, "bfloat16"),
+        ("LR", 2048, "bfloat16"), ("LS", 2048, "bfloat16"), ("ID", 128, "bfloat16"), ("HID", 128, "bfloat16"), ("RA", 256, "float16"),
+        ("LG", 1024, "bfloat16"), ("LG16", 1024, "bfloat16"), ("M16", 16, "bfloat16"), ("BK", 16, "bfloat16"),
+        ("KC", 256, "bfloat16"), ("QC", 240, "bfloat16"), ("C2K", 240, "bfloat16"), ("MSK", 256, "float32"),
+        ("MQ", 256, "bfloat16"), ("CEX", 16, "uint16"), ("gm", 8, "float32"), ("nkp", 1, "float32"),
+        ("pmf", 1, "float32"), ("CJ", 80, "float32"), ("CS", 80, "float32"), ("LANE", 16, "float32"),
+        ("DUM", 80, "float32"), ("WT", 80, "float32"), ("thr", 3, "float32"), ("THR0", 1, "float32"),
+        ("THR1", 1, "float32"), ("CI", 1024, "bfloat16"),
+        ("i0", 256, "int32"), ("i1", 256, "int32"), ("i2", 256, "int32"), ("i3", 256, "int32"), ("i4", 16, "int32"), ("i5", 16, "int32"),
+        ("pc", 1, "int32"), ("pm", 1, "int32"), ("bits", 8, "int32"), ("bf", 8, "float32"), ("a4", 1, "float32"),
+        ("a7", 1, "float32"), ("cf", 256, "float32"),
+        ("ZA", 1280, "bfloat16"), ("GT", 1280, "bfloat16"), ("KL", 96, "bfloat16"),
+        ("VF16", 96, "float16"), ("WF", 96, "float32"), ("VM", 96, "float32"),
+        ("TW", 80, "int32"), ("U", 80, "int32"), ("PEN", 80, "float32"), ("P1", 80, "float32"), ("P2", 80, "float32"),
+        ("P3", 32, "float32"), ("P4", 16, "float32"), ("Q1", 80, "float32"), ("Q2", 80, "float32"), ("Q3", 32, "float32"),
+        ("Q4", 16, "float32"), ("Q5", 16, "int32"), ("QW", 16, "int32"), ("QS", 16, "int32"), ("QZ", 16, "float32"),
+        ("ZO", 16, "uint16"), ("WLU", 16, "uint16"), ("WL", 16, "float32"), ("WL16", 16, "float16"), ("WLM", 16, "float32"),
+        ("BA", 16, "float32"), ("BB", 16, "float32"), ("BC", 16, "float32"), ("BI", 16, "int32"), ("END", 16, "int32"),
+        ("UW", 16, "int32"), ("U16", 16, "float16"), ("W1", 16, "float32"), ("NBD", 16, "float32"), ("WON", 16, "float32"),
+        ("L1", 16, "float32"), ("LE", 16, "float32"), ("CN6", 96, "float32"), ("NC6", 96, "float32"), ("ND6", 96, "float32"),
+        ("VP", 96, "float32"), ("CW6", 96, "float32"), ("CM", 768, "bfloat16"), ("WR", 1, "float32"), ("WRB", 1, "bfloat16"),
+        ("WI", 1, "int32"), ("WI2", 1, "int32"), ("W6", 96, "float32"), ("D6", 96, "float32"),
+        ("OH", 1200, "bfloat16"), ("OHS", 1200, "bfloat16"), ("AB0", 240, "float32"), ("AB1", 240, "float32"),
+        ("VR0", 240, "float16"), ("VR1", 240, "float16"), ("XW", 240, "bfloat16"), ("ZS", 240, "bfloat16"),
+        ("NX", 240, "bfloat16"), ("UP0", 240, "float32"), ("UP1", 240, "float32"), ("T1", 240, "int32"), ("KS", 240, "int32"), ("T2", 240, "int32"),
+        ("T3", 240, "int32"), ("T4", 240, "int32"), ("KF", 4096, "float16"), ("YX", 512, "float32"), ("YK", 512, "float32"),
+        ("WO0", 96, "uint16"), ("WO1", 96, "uint16"), ("ZC0", 240, "bfloat16"), ("ZC1", 240, "bfloat16"),
+        ("PS0", 16, "float32"), ("PS1", 16, "float32"), ("RV0", 128, "float32"), ("RV1", 128, "float32"),
+        ("MI", 96, "int32"), ("F", 96, "int32"), ("BL", 64, "int32"), ("BLW", 32, "int32"), ("OT", 96, "float32"),
+        ("OT2", 96, "float32"), ("OFF", 96, "uint16"), ("EXB", 256, "bfloat16"), ("EXW", 128, "bfloat16"),
+        ("EQ", 6 * 3600, "bfloat16"), ("KVU", 240, "uint16"), ("KVH", 240, "float16"), ("KVC", 240, "float16"),
+        ("XG", 3840, "bfloat16"), ("RX", 3840, "bfloat16"), ("SC", 512, "float32"), ("EX", 384, "bfloat16"),
+        ("XV", 240, "bfloat16"), ("VRS", 240, "float32"), ("DF", 720, "float32"), ("NVM", 96, "float32"), ("ZT", 256, "bfloat16"), ("NID", 128, "bfloat16"), ("NHID", 128, "bfloat16")):
+    _sb(_n, _c, _d)
+for _n, _c in (("ZR0", 1024), ("ZR1", 1024), ("KB0", 512), ("KB1", 512), ("MA", 512), ("MB", 512)):
+    _sb(_n, _c, "float32", "psum")
+QS = ("v", "s", "t", "g")
+DMAS = ("dz", "dv", "dk", "dx", "ox", "ok")
+SEMAPHORES = ["qv", "qs", "qt", "qg"] + list(DMAS) + ["zarr", "parr0", "parr1", "sent"]
+
+
+def build(g, core, T, topo):
+    rank = T.rank_of(core)
+    n = len(T.cores)
+    ops = []
+    hist = {}
+
+    def A(name, a=0, b=None, st=1, p=128, p0=0):
+        home, at, cols = VIEW[name]
+        buf = T[home]
+        b = cols if b is None else b
+        if SCRATCH[home][0] == "psum":
+            reg = [("%s.%d" % (name, k), 0, 1, 1, True) for k in range(a // 512, (b - 1) // 512 + 1)]
+        else:
+            reg = [(name, a, b, st, False)]
+        ap = buf[p0:p, at + a:at + b] if st == 1 else buf[p0:p, at + a:at + b:st]
+        return ap, reg, len(range(a, b, st))
+
+    def IND(win, a, b, off, c, d):
+        return A(win, a, b)[0].indirect(A(off, c, d)[0]), [(win, a, b, 1, False), (off, c, d, 1, False)], 16 * (d - c)
+
+    def add(q, calls, reads, writes, cost, sig=None, kind="c"):
+        i = len(ops)
+        deps = {}
+        for acc, wr in ((reads, False), (writes, True)):
+            for x in acc:
+                for (name, a, b, st, ps) in x[1]:
+                    for (a2, b2, s2, w2, q2, j) in hist.get(name, ()):
+                        if j == i:
+                            continue
+                        if ps:
+                            if q2 != q:
+                                deps[j] = True
+                            else:
+                                deps.setdefault(j, False)
+                            continue
+                        if not (wr or w2) or a >= b2 or a2 >= b:
+                            continue
+                        if st == s2 and st > 1 and (a - a2) % st:
+                            continue
+                        if q2 == q == "t":
+                            deps.setdefault(j, False)
+                        else:
+                            deps[j] = True
+        for acc, wr in ((reads, False), (writes, True)):
+            for x in acc:
+                for (name, a, b, st, ps) in x[1]:
+                    h = hist.setdefault(name, set())
+                    if ps:
+                        h -= {k for k in h if k[4] != q}
+                    elif wr and st == 1:
+                        h -= {k for k in h if k[0] >= a and k[1] <= b and k[5] != i}
+                    h.add((a, b, st, wr, q if kind == "c" else "%s%d" % (q, i), i))
+        ops.append({"q": q, "calls": calls, "deps": deps, "cost": cost, "sig": sig, "kind": kind,
+                    "name": writes[0][1][0][0] if writes else ""})
+        return i
+
+    V, S, PE = g.vector, g.scalar, g.tensor
+
+    def vcost(o, per=1.0, ind=False, sc=False):
+        return (0.06 if not ind else 0.05) + (1.56 if ind and not sc else 3.5 if sc else per) * max(o[2], 1 if ind else 64) * 0.00083
+
+    def cp(o, a, ind=False, sc=False, fast=False):
+        add("v", [lambda: V.tensor_copy(o[0], a[0])], [a], [o], vcost(a if sc else o, 0.5 if fast else 1.0, ind, sc))
+
+    def tt(o, a, b, op, ind=False, two=True):
+        add("v", [lambda: V.tensor_tensor(o[0], a[0], b[0], op)], [a, b], [o], vcost(o, 2.0 if two else 1.0, ind))
+
+    def ts(o, a, s1, op0, s2=None, op1=None, fast=False):
+        r = [a] + [x for x in (s1, s2) if isinstance(x, tuple)]
+        v1 = s1[0] if isinstance(s1, tuple) else s1
+        v2 = s2[0] if isinstance(s2, tuple) else s2
+        if op1 is None:
+            c = lambda: V.tensor_scalar(o[0], a[0], v1, None, op0)
+        else:
+            c = lambda: V.tensor_scalar(o[0], a[0], v1, v2, op0, op1)
+        add("v", [c], r, [o], vcost(o, 0.5 if fast else 1.0))
+
+    def ms(o, val):
+        add("v", [lambda: V.memset(o[0], val)], [], [o], vcost(o, 0.5))
+
+    def act(o, a, func, bias=None, scale=None, ind=False):
+        r = [a] + [x for x in (bias, scale) if isinstance(x, tuple)]
+        kw = {}
+        if bias is not None:
+            kw["bias"] = bias[0] if isinstance(bias, tuple) else bias
+        if scale is not None:
+            kw["scale"] = scale[0] if isinstance(scale, tuple) else scale
+        add("s", [lambda: S.activation(o[0], a[0], func, **kw)], r, [o], 0.08 + (1.56 if ind else 1.0) * o[2] * 0.00083)
+
+    def mm(lst):
+        def one(x):
+            return lambda: PE.matmul(x[0][0], x[1][0], x[2][0], x[3], x[4])
+        add("t", [one(x) for x in lst], [y for x in lst for y in (x[1], x[2])], [x[0] for x in lst],
+            0.06 + sum(max(64, x[0][2]) for x in lst) * 0.0005)
+
+    def group(lst):
+        k = len(lst)
+        mm([(o, a, b, i == 0, i == k - 1) for i, (o, a, b) in enumerate(lst)])
+
+    def dma(q, sem, out, in_, reads, writes, lat):
+        eng = g.sync if q == "y" else g.scalar
+        add(q, [lambda: eng.dma_start(out, in_).then_inc(T.sem[sem], 16)], reads, writes, lat, sig=(sem, 16), kind="d")
+
+    dma("y", "dz", T.zl[:], T.z0[:], [], [A("zl")], 2.0)
+    dma("s", "dv", T.vl[:], T.v0[:], [], [A("vl")], 2.0)
+    dma("y", "dk", T.Kt[:, 0:4096], T.k0[:], [], [A("Kt", 0, 4096)], 8.0)
+    dma("s", "dx", T.Xt[:, 0:4096], T.x0[:], [], [A("Xt", 0, 4096)], 8.0)
+    cp(A("snd", 0, 96), A("zl"), fast=True)
+    ts(A("snd", 96, MSG), A("vl"), -2048.0, OP.add)
+    hosts = [T.cores[(rank + j) % n] for j in range(1, 6)]
+    peers = [T.cores[(rank + d) % n] for d in range(1, n)]
+
+    def dest(c):
+        a = topo.addr(c)
+        return DstId(rid=a[0], pnc=a[1])
+
+    def common(lst):
+        m = topo.mask(core, lst[0])
+        for c in lst:
+            m &= topo.mask(core, c)
+        return m
+    mk = common(peers)
+    ne = bin(mk).count("1")
+    add("g", [lambda: g.remote_dma_fused([RemoteDMATransfer(
+        dst_ids=[dest(c) for c in hosts], dma_engine_mask=mk, remote_sem=T.sem["zarr"], srcs=[T.snd[:]],
+        dsts=[T.land[:, j * MSG:(j + 1) * MSG] for j in range(5)])], local_sem=T.sem["sent"])],
+        [A("snd")], [], 1.0, sig=("sent", ne), kind="r")
+    z_in = add("n", [], [], [], 6.0, kind="n")
+    ops[z_in]["deps"][z_in - 1] = True
+    w = add("v", [lambda: V.wait_ge(T.sem["zarr"], 5 * ne)], [], [A("land")], 0.0, kind="w")
+    ops[w]["deps"][z_in] = False
+
+    def iota(o, pattern, base, ch, flag=False):
+        kw = {"allow_small_or_imprecise_dtypes": True} if flag else {}
+        add("g", [lambda: g.iota(o[0], pattern, base, ch, **kw)], [], [o], 0.13 + 0.00166 * o[2])
+
+    def sel(o, a, pattern, base, ch):
+        add("g", [lambda: g.affine_select(o[0], a[0], pattern, OP.is_equal, 0.0, base, ch)], [a], [o], 0.17 + 0.00166 * o[2])
+    ms(A("ones"), 1.0)
+    sel(A("ID"), A("ones", 0, 128), [[-1, 128]], 0, 1)
+    iota(A("pc"), [[0, 1]], 0, 1)
+    iota(A("i0", 0, 16), [[-1, 16]], 128, 1)
+    iota(A("i1", 0, 16), [[0, 2], [-16, 8]], 0, 1)
+    iota(A("i2"), [[0, 32], [-16, 8]], 0, 1)
+    sel(A("E"), A("ones"), [[-1, 128], [0, 16]], 0, 1)
+    iota(A("i3", 0, 16), [[16, 16]], 0, 0)
+    iota(A("KC"), [[93 * 256, 2], [0, 8], [-256, 16]], 2560, 0, True)
+    ts(A("HID"), A("ID"), 0.5, OP.mult, fast=True)
+    ts(A("NHID"), A("ID"), -0.5, OP.mult, fast=True)
+    ts(A("NID"), A("ID"), -1.0, OP.mult, fast=True)
+    cp(A("RA", 0, 128), A("ID"), fast=True)
+    ts(A("RA", 128, 256), A("ID"), -16.0, OP.mult, fast=True)
+    ms(A("QC"), -0.25)
+    ms(A("C2K"), 2048.0)
+    ms(A("MSK"), 1.0)
+    ms(A("MSK", 0, 256, 16), 0.0)
+    ts(A("pm"), A("pc"), 15, OP.bitwise_and)
+    cp(A("pmf"), A("pm"))
+    ts(A("nkp"), A("pmf"), -15.0, OP.add)
+    ts(A("i4"), A("i0", 0, 16), 15, OP.bitwise_and)
+    ts(A("M16"), A("i4"), 0.0, OP.is_equal)
+    ts(A("i5"), A("i1", 0, 16), 4, OP.arith_shift_right)
+    ts(A("BK"), A("i5"), 0.0, OP.is_equal, 4096.0, OP.mult)
+    ts(A("gm"), A("i5", 0, 8), 0.0, OP.is_equal)
+    ts(A("i0"), A("i2"), 4, OP.arith_shift_right)
+    ts(A("MQ"), A("i0"), 0.0, OP.is_equal)
+    ts(A("LANE"), A("i3", 0, 16), A("pmf"), OP.add)
+    cp(A("i2", 0, 16), A("LANE"))
+    ts(A("i1", 0, 16), A("i2", 0, 16), 3, OP.arith_shift_right)
+    cp(A("CEX"), A("i1", 0, 16))
+    for x in range(6):
+        ts(A("D6", 16 * x, 16 * x + 16), A("LANE"), 4096.0, OP.add)
+    ms(A("LG"), 0.0)
+    ms(A("LG16"), 0.0)
+    for x in range(8):
+        cp(A("LG", 144 * x, 144 * x + 16), A("M16"))
+        ts(A("LG16", 144 * x, 144 * x + 16), A("M16"), 16.0, OP.mult)
+    ms(A("LS"), 0.0)
+    for r in range(16):
+        cp(A("LS", 129 * r, 128 * r + 128, 16), A("gm"))
+    ms(A("F"), 0)
+    ms(A("BL"), 0)
+    ms(A("BLW"), 0)
+    ms(A("WO0"), 0)
+    ms(A("WO1"), 0)
+    ms(A("GT"), 0.0)
+    ms(A("ZA"), 0.0)
+    ms(A("KL"), 0.0)
+    ms(A("THR0"), 6.0)
+    sel(A("LR"), A("ones"), [[-1, 16], [-16, 8], [0, 16]], 0, 1)
+    for s in range(5):
+        iota(A("cf", 16 * s, 16 * s + 15), [[1, 5], [0, 3]], 8 * (s + 1) + 1, 0, True)
+    iota(A("cf", 96, 176), [[1, 5], [0, 16]], 1, 0, True)
+    ms(A("CJ"), 0.0)
+    for s in range(5):
+        ts(A("CJ", 16 * s, 16 * s + 15), A("cf", 16 * s, 16 * s + 15), 4096.0, OP.mult)
+    ts(A("CS"), A("cf", 96, 176), 4096.0, OP.mult)
+    for i in range(7):
+        ts(A("bits", i, i + 1), A("pc"), i, OP.arith_shift_right, 1, OP.bitwise_and)
+        ts(A("bf", i, i + 1), A("bits", i, i + 1), 0.0, OP.is_equal, 2.0 ** -(1 << i), OP.max)
+    tt(A("a4"), A("bf", 0, 1), A("bf", 1, 2), OP.mult)
+    tt(A("a4"), A("a4"), A("bf", 2, 3), OP.mult)
+    tt(A("a4"), A("a4"), A("bf", 3, 4), OP.mult)
+    ts(A("a7"), A("a4"), 2.0 ** 60, OP.mult, A("bf", 4, 5), OP.mult)
+    tt(A("a7"), A("a7"), A("bf", 5, 6), OP.mult)
+    tt(A("a7"), A("a7"), A("bf", 6, 7), OP.mult)
+    for b in range(NB):
+        ts(A("thr", b, b + 1), A("a7"), 2.0 ** (60 - 128 * b), OP.mult)
+    ms(A("cf", 176, 192), 0.0)
+    for c in range(15):
+        ms(A("cf", 176 + c, 177 + c), 2.0 ** (99 - 16 * c))
+    ts(A("a4"), A("a4"), 2.0 ** 20, OP.mult)
+    for x in range(6):
+        ts(A("W6", 16 * x, 16 * x + 16), A("cf", 176, 192), A("a4"), OP.mult)
+    for e in range(6):
+        for q in range(15):
+            lo = 128 * (q // 8)
+            if 16 * q > lo:
+                iota(A("EQ", e * 3600 + 240 * q + lo, e * 3600 + 256 * q), [[0, 16 * q - lo]], 0, 0, True)
+    for a in range(8):
+        ts(A("CI", 128 * a, 128 * a + 128), A("ID"), float(a + 1), OP.mult, fast=True)
+
+    for t in range(2):
+        wo, zc, ps, rv, par = "WO%d" % t, "ZC%d" % t, "PS%d" % t, "RV%d" % t, "parr%d" % t
+        for j in range(5):
+            o = j * MSG
+            ts(A(wo, 3 * j, 3 * j + 3), A("land", o + 96 + t * 15 + 3 * j, o + 99 + t * 15 + 3 * j), 2048.0, OP.add)
+            cp(A(zc, 48 * j, 48 * j + 48), A("land", o + t * 48, o + t * 48 + 48), fast=True)
+
+        def zturn(b, z):
+            mm([(A("MA", 128, 256, p=LN[b]), z, A("ID"), True, True)])
+            act(A("ZT", 128 * b, 128 * b + 128, p=LN[b]), A("MA", 128, 256, p=LN[b]), AF.Copy)
+        for b in range(NB):
+            zturn(b, A(zc, 128 * b, 128 * b + LN[b]))
+        for s in range(1, 6):
+            for b in range(NB):
+                nl, nq = LN[b], LN[b] // 16
+                l0, c0, u0 = (s - 1) * 16 + 8 * b, s * 16 + 8 * b, 128 * b
+                kb = "KB%d" % b
+                z = A(zc, u0, u0 + nl) if s == 1 else A("ZA", (s - 2) * 256 + u0, (s - 2) * 256 + u0 + nl)
+                cp(A("KVU", u0, u0 + nl), IND("Kt", 0, 4096, wo, l0, l0 + nq), ind=True)
+                zt = A("ZT", u0, u0 + 128, p=nl)
+                for h, (a, e) in enumerate(CHUNKS[b]):
+                    x0, x1 = 16 * (u0 + a), 16 * (u0 + e)
+                    zr, w = "ZR%d" % (h % 2), 16 * (e - a)
+                    act(A("XG", x0, x1), IND("Xt", 0, 4096, "KVU", u0 + a, u0 + e), AF.Copy, ind=True)
+                    cuts = [(k, min(k + 512, w)) for k in range(0, w, 512)]
+                    if (b, h) in ON_S:
+                        for k, m in cuts:
+                            group([(A(zr, k, m), zt, A("E", 16 * a + k, 16 * a + m, p=nl)), (A(zr, k, m), A("NID"), A("XG", x0 + k, x0 + m))])
+                        act(A("RX", x0, x1), A(zr, 0, w), AF.Relu, scale=-1.0)
+                    else:
+                        mm([(A(zr, k, m), zt, A("E", 16 * a + k, 16 * a + m, p=nl), True, True) for k, m in cuts])
+                        tt(A("RX", x0, x1), A("XG", x0, x1), A(zr, 0, w), OP.max, two=False)
+                ts(A("KVH", u0, u0 + nl), A("KVU", u0, u0 + nl), 1.0 / 16, OP.mult, 1280.0 - 15.0 / 32, OP.add, fast=True)
+                ts(A("KVC", u0, u0 + nl), A("KVU", u0, u0 + nl), -2048.0, OP.add, fast=True)
+                lst = [(A(kb, 0, 256, p=nl), A("ones", 0, nl, p=1), A("KC", p=1)),
+                       (A(kb, 128, 256, p=nl), A("KVC", u0, u0 + nl), A("RA", 0, 128)),
+                       (A(kb, 0, 256, p=nl), A("KVH", u0, u0 + nl), A("RA"))]
+                for k in range(16):
+                    lst.append((A(kb, k, 256, 16, p=nl), A("RX", 16 * u0 + k, 16 * (u0 + nl), 16), A("BK")))
+                group(lst)
+                sc, mi, f, ex = 256 * b, 32 * b, 32 * b, 192 * b
+                o = A("SC", sc, sc + 256, p=nl)
+                m_, kk = A("MSK", p=nl), A(kb, 0, 256, p=nl)
+                add("v", [lambda o=o, m_=m_, kk=kk: V.tensor_tensor_scan(o[0], m_[0], kk[0], 0.0, OP.mult, OP.max)],
+                    [m_, kk], [o], vcost(o))
+                cp(A("MI", mi, mi + 16, p=nl), A("SC", sc + 15, sc + 256, 16, p=nl))
+                ts(A("F", f, f + 8, p=nl), A("MI", mi, mi + 8, p=nl), 255, OP.bitwise_and)
+                ts(A("F", f + 8, f + 24, 2, p=nl), A("MI", mi + 8, mi + 16, p=nl), 255, OP.bitwise_and)
+                ts(A("F", f + 9, f + 24, 2, p=nl), A("MI", mi, mi + 8, p=nl), 8, OP.arith_shift_right, 15, OP.bitwise_and)
+                tt(A("EX", ex, ex + 192), IND("F", f, f + 32, "CEX", 0, 12), A("MQ", 0, 192), OP.mult, ind=True)
+                lst = []
+                for x in range(8):
+                    e = ex + 64 + 16 * x
+                    lst.append((A("MB", 0, 16), A("LG", 128 * x, 128 * x + 128, p=nl), A("EX", e, e + 16, p=nl)))
+                    e = ex + 8 * x
+                    lst.append((A("MB", 0, 8), A("LG16", 128 * x, 128 * x + 128, p=nl), A("EX", e, e + 8, p=nl)))
+                group(lst)
+                cp(A(wo, c0, c0 + 8), A("MB", 0, 8))
+                act(A("KL", c0, c0 + 8), A("MB", 8, 16), AF.Copy)
+                act(A("XV", u0, u0 + nl), IND("Xt", 0, 4096, wo, c0, c0 + nq), AF.Copy, ind=True)
+                cq = (A("ones", 0, 128, p=1), A("QC", 0, nl, p=1))
+                ma, md = A("MA", 0, nl), A("MA", 256, 256 + nl)
+                xv = A("XV", u0, u0 + nl)
+                group([(ma, cq[0], cq[1]), (ma, A("HID"), z), (ma, A("HID"), xv)])
+                group([(md, cq[0], cq[1]), (md, A("NHID"), z), (md, A("HID"), xv)])
+                zo = (s - 1) * 256 + u0
+                ts(A("ZA", zo, zo + nl), ma, MAG, OP.add, -MAG, OP.add)
+                if s < 5:
+                    zturn(b, A("ZA", zo, zo + nl))
+                act(A("GT", zo, zo + nl), md, AF.Sign)
+            if s in (4, 5):
+                a, m = (0, 64) if s == 4 else (64, 16)
+                for off, src in ((64, "GT"), (160, "ZA")):
+                    group([(A("MB", off + a, off + a + m), A("LS", 128 * r, 128 * r + 128),
+                            A(src, 16 * a + r, 16 * (a + m), 16)) for r in range(16)])
+            if s == 4:
+                ts(A("VF16", 0, 80), A(wo, 0, 80), -2048.0, OP.add)
+                ts(A("VM", 0, 80), A(wo, 0, 80), -2048.0, OP.add)
+        cp(A("WF"), A(wo))
+        tt(A("TW"), A("WF", 16, 96), A("MB", 160, 240), OP.mult, two=False)
+        ts(A("U"), A("TW"), 4095, OP.bitwise_and)
+        ts(A("PEN"), A("MB", 64, 144), A("THR%d" % t), OP.is_lt, BIG, OP.mult)
+        tt(A("P1"), A("U"), A("CJ"), OP.add)
+        tt(A("P2"), A("P1"), A("PEN"), OP.add)
+        tt(A("P3"), A("P2", 0, 32), A("P2", 32, 64), OP.min)
+        tt(A("P4"), A("P3", 0, 16), A("P3", 16, 32), OP.min)
+        tt(A(ps), A("P4"), A("P2", 64, 80), OP.min)
+        add("g", [lambda ps=ps, rv=rv, par=par: g.remote_dma_fused([RemoteDMATransfer(
+            dst_ids=[dest(c) for c in peers], dma_engine_mask=mk, remote_sem=T.sem[par], srcs=[T[ps][:]],
+            dsts=[T[rv][:, 16 * rank:16 * rank + 16] for c in peers])], local_sem=T.sem["sent"])],
+            [A(ps)], [], 1.0, sig=("sent", ne * (t + 2)), kind="r")
+        p_in = add("n", [], [], [], 5.0, kind="n")
+        ops[p_in]["deps"][p_in - 1] = True
+        tt(A("Q1"), A("WF", 16, 96), A("CS"), OP.add)
+        tt(A("Q2"), A("Q1"), A("PEN"), OP.add)
+        tt(A("Q3"), A("Q2", 0, 32), A("Q2", 32, 64), OP.min)
+        tt(A("Q4"), A("Q3", 0, 16), A("Q3", 16, 32), OP.min)
+        tt(A("Q5"), A("Q4"), A("Q2", 64, 80), OP.min)
+        ts(A("QW"), A("Q5"), 4095, OP.bitwise_and)
+        ts(A("QS"), A("Q5"), 12, OP.arith_shift_right)
+        cp(A("WF", 80, 96), A("QW"))
+        cp(A("WLU"), A("QW"))
+        ts(A("VF16", 80, 96), A("QW"), -2048.0, OP.add)
+        ts(A("VM", 80, 96), A("QW"), -2048.0, OP.add)
+        ts(A("NVM"), A("VM"), -1.0, OP.mult)
+        ts(A("QZ"), A("QS"), 5.0, OP.min, 256.0, OP.mult)
+        tt(A("QZ"), A("QZ"), A("LANE"), OP.add)
+        ts(A("ZO"), A("QZ"), -256.0, OP.add)
+        act(A("XW"), IND("Xt", 0, 4096, "WLU", 0, 15), AF.Copy, ind=True)
+        act(A("ZS"), IND("ZA", 0, 1280, "ZO", 0, 15), AF.Copy, ind=True)
+
+        def rows(out, src, a):
+            mm([(A(out[0], out[1] + r, out[1] + 240, 16), A("LR", 128 * r, 128 * r + 128), A(src, a, a + 15), True, True)
+                for r in range(16)])
+        for i, e in enumerate((4, 3, 2, 1, 0, 5)):
+            rows(("KB0", 256), "VF16", 16 * e)
+            vr = "VR%d" % (i % 2)
+            if e in EQ_S:
+                act(A("VRS"), A("KB0", 256, 496), AF.Copy)
+            else:
+                cp(A(vr), A("KB0", 256, 496))
+            for q in range(15):
+                eq, col = A("EQ", e * 3600 + 256 * q, e * 3600 + 240 * q + 240), (16 * e + q, 16 * e + q + 1)
+                if e in EQ_S:
+                    df = A("DF", 240 * (q % 3), 240 * (q % 3) + 240 - 16 * q)
+                    act(df, A("VRS", 16 * q, 240), AF.Abs, bias=A("NVM", *col))
+                    act(eq, df, AF.Relu, bias=1.0, scale=-1.0)
+                else:
+                    ts(eq, A(vr, 16 * q, 240), A("VM", *col), OP.is_equal, fast=True)
+            if e < 5:
+                s = e + 1
+                rows(("KB1", 256), "KL", 16 * s)
+                ab = "AB%d" % (i % 2)
+                act(A(ab), A("KB1", 256, 496), AF.Abs, bias=A("nkp"))
+                act(A("OH", 240 * e, 240 * e + 240), A(ab), AF.Relu, bias=1.0, scale=-1.0)
+                act(A("OHS", 240 * e, 240 * e + 240), A(ab), AF.Relu, bias=float(s), scale=-float(s))
+        group([(A("ZR1", 512, 752), A("ones", 0, 128, p=1), A("QC", p=1)), (A("ZR1", 512, 752), A("HID"), A("XW")),
+               (A("ZR1", 512, 752), A("HID"), A("ZS"))])
+        ts(A("NX"), A("ZR1", 512, 752), MAG, OP.add, -MAG, OP.add)
+        w = add("v", [lambda par=par: V.wait_ge(T.sem[par], (n - 1) * ne)], [], [A(rv)], 0.0, kind="w")
+        ops[w]["deps"][p_in] = False
+        for acc, ds in (("BA", (1, 2, 3, 4)), ("BB", (-1, -2, -3, -4))):
+            cp(A(acc), A(ps))
+            for d in ds:
+                lo, hi = max(0, -d), min(5, 5 - d)
+                o = 16 * ((rank + d) % n)
+                tt(A(acc, 3 * lo, 3 * hi), A(acc, 3 * lo, 3 * hi), A(rv, o + 3 * (lo + d), o + 3 * (hi + d)), OP.min)
+        tt(A("BC"), A("BA"), A("BB"), OP.min)
+        cp(A("BI"), A("BC"))
+        ts(A("UW"), A("BI"), 4095, OP.bitwise_and)
+        ts(A("END"), A("BI"), 15, OP.arith_shift_right)
+        ts(A("U16"), A("UW"), -2048.0, OP.add)
+        tt(A("W1"), A("BC"), A(ps), OP.is_equal)
+        ts(A("NBD"), A("BC"), BIG, OP.is_lt)
+        tt(A("WON"), A("W1"), A("NBD"), OP.mult)
+        tt(A("L1"), A("NBD"), A("WON"), OP.subtract)
+        tt(A("LE"), A("END"), A("L1"), OP.mult)
+        for s in range(1, 6):
+            ts(A("CN6", 16 * s - 16, 16 * s), A("LE"), float(s), OP.is_ge)
+        cp(A("CN6", 80, 96), A("WON"))
+        tt(A("CW6"), A("CN6"), A("W6"), OP.mult)
+        for x in range(8):
+            if x < 4:
+                ts(A("CM", x, 768, 8), A("CW6"), A("gm", x, x + 1), OP.mult)
+            else:
+                act(A("CM", x, 768, 8), A("CW6"), AF.Copy, scale=A("gm", x, x + 1))
+        ts(A("NC6"), A("CN6"), -1.0, OP.mult, 1.0, OP.add)
+        tt(A("ND6"), A("NC6"), A("D6"), OP.mult)
+        tt(A("VP"), A("ND6"), A("WF"), OP.max)
+        group([(A("ZR1", 0, 240), A("ones", 0, 128, p=1), A("C2K", p=1))] +
+              [(A("ZR1", r, 240, 16), A("LR", 128 * r, 128 * r + 128), A("U16", 0, 15)) for r in range(16)])
+
+        def lowest(es, bl, ex):
+            for i, e in enumerate(es):
+                for b in range(NB):
+                    group([(A("ZR0", 16 * i + b, 16 * i + 16, 2, p=LN[b]),
+                            A("EQ", e * 3600 + 240 * q + 128 * b, e * 3600 + 240 * q + 128 * b + LN[b]),
+                            A("CM", (16 * e + q) * 8, (16 * e + q) * 8 + 8)) for q in range((8, 15)[b])])
+            k = len(es)
+            for b in range(NB):
+                ts(A(bl, b, 16 * k, 2, p=LN[b]), A("ZR0", b, 16 * k, 2, p=LN[b]), A("thr", b, b + 1, p=LN[b]), OP.is_ge)
+            tt(A(ex, 0, 128 * k), IND(bl, 0, 16 * k, "CEX", 0, 8 * k), A("MQ", 0, 128 * k), OP.mult, ind=True)
+            for i, e in enumerate(es):
+                group([(A("ZR0", 512 + 16 * i, 527 + 16 * i), A("LG", 128 * x, 128 * x + 128),
+                        A(ex, 128 * i + 16 * x, 128 * i + 16 * x + 15)) for x in range(8)])
+            for i, e in enumerate(es):
+                c = 16 * e
+                tt(A("OT", c, c + 15), A("ZR0", 512 + 16 * i, 527 + 16 * i), A("D6", c, c + 15), OP.mult, two=False)
+                tt(A("OT2", c, c + 15), A("OT", c, c + 15), A("VP", c, c + 15), OP.max)
+                cp(A("OFF", c, c + 15), A("OT2", c, c + 15))
+
+        def change(e):
+            up = "UP%d" % (e % 2)
+            tt(A(up), A("OH", 240 * e, 240 * e + 240), A("ZR1", 0, 240), OP.mult, two=False)
+            lw = IND("Kt", 0, 4096, wo, 16 * e, 16 * e + 15)
+            tt(A("T1"), lw, A(up), OP.mult, ind=True)
+            tt(A("KS"), lw, A("OHS", 240 * e, 240 * e + 240), OP.add, ind=True)
+            ts(A("T2"), A("T1"), 5, OP.arith_shift_right)
+            tt(A("T3"), A("T2"), A("KS"), OP.add)
+            ts(A("T4"), A("T3"), 4095, OP.bitwise_and)
+            o = IND("Kt", 0, 4352, "OFF", 16 * e, 16 * e + 15)
+            a = A("T4")
+            add("v", [lambda: V.tensor_copy(o[0], a[0])], [a, (None, [o[1][1]], 0)], [(None, [o[1][0]], 0)], vcost(a, 1.0, True, True))
+        lowest((4,), "BLW", "EXW")
+        lowest((3, 2), "BL", "EXB")
+        change(4)
+        lowest((1, 0), "BL", "EXB")
+        change(3)
+        lowest((5,), "BLW", "EXW")
+        change(2)
+        o = IND("Xt", 0, 4352, "OFF", 80, 95)
+        a = A("NX")
+        add("v", [lambda o=o, a=a: V.tensor_copy(o[0], a[0])], [a, (None, [o[1][1]], 0)], [(None, [o[1][0]], 0)], vcost(a, 1.0, True, True))
+        change(1)
+        change(0)
+        if t == 0:
+            add("v", [lambda: V.tensor_reduce(A("WR")[0], A("WON")[0], AxisListType.X, OP.add)], [A("WON")], [A("WR")], 0.11)
+            cp(A("WRB"), A("WR"))
+            mm([(A("MA", 300, 301), A("ones", 0, 128), A("WRB"), True, True)])
+            cp(A("WI"), A("MA", 300, 301))
+            ts(A("WI2"), A("WI"), 1, OP.bitwise_and)
+            ts(A("THR1"), A("WI2"), 2.0, OP.mult, 6.0, OP.add)
+    group([(A("MA"), A("CI", 128 * a, 128 * a + 128), A("Xt", 512 * a, 512 * a + 512)) for a in range(8)])
+    act(A("YX"), A("MA"), AF.Copy)
+    dma("s", "ox", T.yx[:], T.YX[:], [A("YX")], [], 2.0)
+    for a in range(8):
+        ts(A("KF", 512 * a, 512 * a + 512), A("Kt", 512 * a, 512 * a + 512), -2048.0, OP.add)
+    for a in range(8):
+        mm([(A("MB"), A("CI", 128 * a, 128 * a + 128), A("KF", 512 * a, 512 * a + 512), a == 0, a == 7)])
+    ts(A("YK"), A("MB"), 36.0 * 2048.0, OP.add)
+    dma("y", "ok", T.yk[:], T.YK[:], [A("YK")], [], 2.0)
+    return ops, ne
+
+
+def order(ops):
+    k = len(ops)
+    succ = [[] for _ in range(k)]
+    for i, o in enumerate(ops):
+        for d in o["deps"]:
+            succ[d].append(i)
+    lat = 0.1
+    prio = [0.0] * k
+    for i in range(k - 1, -1, -1):
+        prio[i] = ops[i]["cost"] + max([prio[j] + lat for j in succ[i]] or [0.0])
+    left = [len(o["deps"]) for o in ops]
+    at = [0.0] * k
+    free = {}
+    pool = {}
+    for i in range(k):
+        if not left[i]:
+            pool.setdefault(ops[i]["q"], []).append(i)
+    done = []
+    for _ in range(k):
+        best = None
+        for q, c in pool.items():
+            if not c:
+                continue
+            f = free.get(q, 0.0)
+            st = max(f, min(at[i] for i in c))
+            i = max((i for i in c if at[i] <= st + 1e-9), key=lambda i: prio[i] - 0.01 * i)
+            if best is None or st < best[0]:
+                best = (st, q, i)
+        st, q, i = best
+        pool[q].remove(i)
+        o = ops[i]
+        free[q] = st + (0.1 if o["kind"] == "d" else 0.0 if o["kind"] == "n" else o["cost"])
+        end = st + o["cost"]
+        done.append(i)
+        for j in succ[i]:
+            at[j] = max(at[j], end + (lat if o["kind"] != "w" else 0.0))
+            left[j] -= 1
+            if not left[j]:
+                pool.setdefault(ops[j]["q"], []).append(j)
+    return done
+
+
+def emit(g, T, ops, seq, ne):
+    eng = {"v": g.vector, "s": g.scalar, "t": g.tensor, "g": g, "y": g.sync}
+    count = {q: 0 for q in QS}
+    known = {q: {} for q in eng}
+    clock = {}
+    sig = {}
+    for i in seq:
+        o = ops[i]
+        q = o["q"]
+        if o["kind"] == "n":
+            continue
+        need = {}
+        for d, must in o["deps"].items():
+            if must and d in sig:
+                sem, val = sig[d]
+                if known[q].get(sem, 0) < val:
+                    need[sem] = max(need.get(sem, 0), val)
+        for sem in sorted(need, key=lambda x: -len(clock[(x, need[x])])):
+            if known[q].get(sem, 0) >= need[sem]:
+                continue
+            eng[q].wait_ge(T.sem[sem], need[sem])
+            known[q][sem] = need[sem]
+            for s2, v2 in clock[(sem, need[sem])].items():
+                if known[q].get(s2, 0) < v2:
+                    known[q][s2] = v2
+        for c in o["calls"][:-1]:
+            c()
+        last = o["calls"][-1]()
+        if o["kind"] == "c":
+            count[q] += 1
+            sem = "q" + q
+            last.then_inc(T.sem[sem], 1)
+            sig[i] = (sem, count[q])
+            clock[(sem, count[q])] = dict(known[q])
+        elif o["kind"] in ("d", "r"):
+            sig[i] = o["sig"]
+            clock[o["sig"]] = dict(known[q])
+    for q in QS:
+        if count[q]:
+            g.wait_ge(T.sem["q" + q], count[q])
+    for s in DMAS:
+        g.wait_ge(T.sem[s], 16)
+    g.wait_ge(T.sem["sent"], 3 * ne)
+
+
+def rank_program(g, core, T, topo):
+    if T.rank_of(core) is None:
+        return
+    ops, ne = build(g, core, T, topo)
+    emit(g, T, ops, order(ops), ne)

@@ -5,9 +5,13 @@ from concourse.mybir import AluOpType, AxisListType, ActivationFunctionType
 OP = AluOpType
 AF = ActivationFunctionType
 NB, LN = 2, (128, 112)
+QB, QN = (0, 8), (8, 7)
+ALPHA, KS_PE = 0.02, True
+ZBUF = (("ZR0", 0), ("ZR1", 0))
 CHUNKS = (((0, 32), (32, 64), (64, 96), (96, 128)), ((0, 32), (32, 64), (64, 96), (96, 112)))
-ON_S = ((0, 3),)
-EQ_S = (1, 0, 5)
+ON_S = ()
+ON_V = ("KL", "GT", "ZT")
+EQ_S = (0, 5)
 BIG = 1048576.0
 MAG = 8388608.0
 MSG = 126
@@ -62,8 +66,8 @@ for _n, _c, _d in (
         ("MI", 96, "int32"), ("F", 96, "int32"), ("BL", 64, "int32"), ("BLW", 32, "int32"), ("OT", 96, "float32"),
         ("OT2", 96, "float32"), ("OFF", 96, "uint16"), ("EXB", 256, "bfloat16"), ("EXW", 128, "bfloat16"),
         ("EQ", 6 * 3600, "bfloat16"), ("KVU", 240, "uint16"), ("KVH", 240, "float16"), ("KVC", 240, "float16"),
-        ("XG", 3840, "bfloat16"), ("RX", 3840, "bfloat16"), ("SC", 512, "float32"), ("EX", 384, "bfloat16"),
-        ("XV", 240, "bfloat16"), ("VRS", 240, "float32"), ("DF", 720, "float32"), ("NVM", 96, "float32"), ("ZT", 256, "bfloat16"), ("NID", 128, "bfloat16"), ("NHID", 128, "bfloat16")):
+        ("XG", 3840, "bfloat16"), ("RX", 3840, "bfloat16"), ("SC", 768, "float32"), ("EX", 576, "bfloat16"),
+        ("XV", 240, "bfloat16"), ("VRS", 240, "float32"), ("IDF", 128, "float32"), ("KSF", 240, "float32"), ("DF", 720, "float32"), ("NVM", 96, "float32"), ("ZT", 384, "bfloat16"), ("NID", 128, "bfloat16"), ("NHID", 128, "bfloat16")):
     _sb(_n, _c, _d)
 for _n, _c in (("ZR0", 1024), ("ZR1", 1024), ("KB0", 512), ("KB1", 512), ("MA", 512), ("MB", 512)):
     _sb(_n, _c, "float32", "psum")
@@ -129,9 +133,10 @@ def build(g, core, T, topo):
         return i
 
     V, S, PE = g.vector, g.scalar, g.tensor
+    T0 = 22.0 if "GT" in ON_V else 6.0
 
     def vcost(o, per=1.0, ind=False, sc=False):
-        return (0.06 if not ind else 0.05) + (1.56 if ind and not sc else 3.5 if sc else per) * max(o[2], 1 if ind else 64) * 0.00083
+        return (0.03 if not ind else 0.05) + (1.56 if ind and not sc else 3.5 if sc else per) * max(o[2], 1 if ind else 64) * 0.00083
 
     def cp(o, a, ind=False, sc=False, fast=False):
         add("v", [lambda: V.tensor_copy(o[0], a[0])], [a], [o], vcost(a if sc else o, 0.5 if fast else 1.0, ind, sc))
@@ -159,13 +164,19 @@ def build(g, core, T, topo):
             kw["bias"] = bias[0] if isinstance(bias, tuple) else bias
         if scale is not None:
             kw["scale"] = scale[0] if isinstance(scale, tuple) else scale
-        add("s", [lambda: S.activation(o[0], a[0], func, **kw)], r, [o], 0.08 + (1.56 if ind else 1.0) * o[2] * 0.00083)
+        add("s", [lambda: S.activation(o[0], a[0], func, **kw)], r, [o], 0.05 + (1.56 if ind else 1.0) * o[2] * 0.00083)
+
+    def copy(what, o, a, ind=False):
+        if what in ON_V:
+            cp(o, a, ind=ind)
+        else:
+            act(o, a, AF.Copy, ind=ind)
 
     def mm(lst):
         def one(x):
             return lambda: PE.matmul(x[0][0], x[1][0], x[2][0], x[3], x[4])
         add("t", [one(x) for x in lst], [y for x in lst for y in (x[1], x[2])], [x[0] for x in lst],
-            0.06 + sum(max(64, x[0][2]) for x in lst) * 0.0005)
+            sum(max(64, x[0][2]) for x in lst) * 0.000417)
 
     def group(lst):
         k = len(lst)
@@ -219,6 +230,7 @@ def build(g, core, T, topo):
     sel(A("E"), A("ones"), [[-1, 128], [0, 16]], 0, 1)
     iota(A("i3", 0, 16), [[16, 16]], 0, 0)
     iota(A("KC"), [[93 * 256, 2], [0, 8], [-256, 16]], 2560, 0, True)
+    cp(A("IDF"), A("ID"))
     ts(A("HID"), A("ID"), 0.5, OP.mult, fast=True)
     ts(A("NHID"), A("ID"), -0.5, OP.mult, fast=True)
     ts(A("NID"), A("ID"), -1.0, OP.mult, fast=True)
@@ -260,7 +272,7 @@ def build(g, core, T, topo):
     ms(A("GT"), 0.0)
     ms(A("ZA"), 0.0)
     ms(A("KL"), 0.0)
-    ms(A("THR0"), 6.0)
+    ms(A("THR0"), T0)
     sel(A("LR"), A("ones"), [[-1, 16], [-16, 8], [0, 16]], 0, 1)
     for s in range(5):
         iota(A("cf", 16 * s, 16 * s + 15), [[1, 5], [0, 3]], 8 * (s + 1) + 1, 0, True)
@@ -302,38 +314,42 @@ def build(g, core, T, topo):
             cp(A(zc, 48 * j, 48 * j + 48), A("land", o + t * 48, o + t * 48 + 48), fast=True)
 
         def zturn(b, z):
-            mm([(A("MA", 128, 256, p=LN[b]), z, A("ID"), True, True)])
-            act(A("ZT", 128 * b, 128 * b + 128, p=LN[b]), A("MA", 128, 256, p=LN[b]), AF.Copy)
-        for b in range(NB):
-            zturn(b, A(zc, 128 * b, 128 * b + LN[b]))
+            m = 16 * QN[b]
+            mm([(A("MA", 128, 256, p=m), z, A("ID"), True, True)])
+            copy("ZT", A("ZT", 128 * b, 128 * b + 128, p=m), A("MA", 128, 256, p=m))
+        for b in range(len(QB)):
+            zturn(b, A(zc, 16 * QB[b], 16 * (QB[b] + QN[b])))
+        nb, nch = 0, 0
         for s in range(1, 6):
-            for b in range(NB):
-                nl, nq = LN[b], LN[b] // 16
-                l0, c0, u0 = (s - 1) * 16 + 8 * b, s * 16 + 8 * b, 128 * b
-                kb = "KB%d" % b
+            for b in range(len(QB)):
+                nl, nq = 16 * QN[b], QN[b]
+                l0, c0, u0 = (s - 1) * 16 + QB[b], s * 16 + QB[b], 16 * QB[b]
+                kb = "KB%d" % (nb % 2)
+                nb += 1
                 z = A(zc, u0, u0 + nl) if s == 1 else A("ZA", (s - 2) * 256 + u0, (s - 2) * 256 + u0 + nl)
                 cp(A("KVU", u0, u0 + nl), IND("Kt", 0, 4096, wo, l0, l0 + nq), ind=True)
-                zt = A("ZT", u0, u0 + 128, p=nl)
+                zt = A("ZT", 128 * b, 128 * b + 128, p=nl)
                 for h, (a, e) in enumerate(CHUNKS[b]):
                     x0, x1 = 16 * (u0 + a), 16 * (u0 + e)
-                    zr, w = "ZR%d" % (h % 2), 16 * (e - a)
-                    act(A("XG", x0, x1), IND("Xt", 0, 4096, "KVU", u0 + a, u0 + e), AF.Copy, ind=True)
+                    zr, z0, w = ZBUF[nch % len(ZBUF)] + (16 * (e - a),)
+                    nch += 1
+                    copy(("XG", b, h), A("XG", x0, x1), IND("Xt", 0, 4096, "KVU", u0 + a, u0 + e), True)
                     cuts = [(k, min(k + 512, w)) for k in range(0, w, 512)]
                     if (b, h) in ON_S:
                         for k, m in cuts:
-                            group([(A(zr, k, m), zt, A("E", 16 * a + k, 16 * a + m, p=nl)), (A(zr, k, m), A("NID"), A("XG", x0 + k, x0 + m))])
-                        act(A("RX", x0, x1), A(zr, 0, w), AF.Relu, scale=-1.0)
+                            zk = A(zr, z0 + k, z0 + m)
+                            group([(zk, zt, A("E", 16 * a + k, 16 * a + m, p=nl)), (zk, A("NID"), A("XG", x0 + k, x0 + m))])
+                        act(A("RX", x0, x1), A(zr, z0, z0 + w), AF.Relu, scale=-1.0)
                     else:
-                        mm([(A(zr, k, m), zt, A("E", 16 * a + k, 16 * a + m, p=nl), True, True) for k, m in cuts])
-                        tt(A("RX", x0, x1), A("XG", x0, x1), A(zr, 0, w), OP.max, two=False)
+                        mm([(A(zr, z0 + k, z0 + m), zt, A("E", 16 * a + k, 16 * a + m, p=nl), True, True) for k, m in cuts])
+                        tt(A("RX", x0, x1), A("XG", x0, x1), A(zr, z0, z0 + w), OP.max, two=False)
                 ts(A("KVH", u0, u0 + nl), A("KVU", u0, u0 + nl), 1.0 / 16, OP.mult, 1280.0 - 15.0 / 32, OP.add, fast=True)
                 ts(A("KVC", u0, u0 + nl), A("KVU", u0, u0 + nl), -2048.0, OP.add, fast=True)
                 lst = [(A(kb, 0, 256, p=nl), A("ones", 0, nl, p=1), A("KC", p=1)),
                        (A(kb, 128, 256, p=nl), A("KVC", u0, u0 + nl), A("RA", 0, 128)),
                        (A(kb, 0, 256, p=nl), A("KVH", u0, u0 + nl), A("RA"))]
-                for k in range(16):
-                    lst.append((A(kb, k, 256, 16, p=nl), A("RX", 16 * u0 + k, 16 * (u0 + nl), 16), A("BK")))
-                group(lst)
+                mm([x + (i == 0, False) for i, x in enumerate(lst)])
+                mm([(A(kb, k, 256, 16, p=nl), A("RX", 16 * u0 + k, 16 * (u0 + nl), 16), A("BK"), False, k == 15) for k in range(16)])
                 sc, mi, f, ex = 256 * b, 32 * b, 32 * b, 192 * b
                 o = A("SC", sc, sc + 256, p=nl)
                 m_, kk = A("MSK", p=nl), A(kb, 0, 256, p=nl)
@@ -351,9 +367,9 @@ def build(g, core, T, topo):
                     e = ex + 8 * x
                     lst.append((A("MB", 0, 8), A("LG16", 128 * x, 128 * x + 128, p=nl), A("EX", e, e + 8, p=nl)))
                 group(lst)
-                cp(A(wo, c0, c0 + 8), A("MB", 0, 8))
-                act(A("KL", c0, c0 + 8), A("MB", 8, 16), AF.Copy)
-                act(A("XV", u0, u0 + nl), IND("Xt", 0, 4096, wo, c0, c0 + nq), AF.Copy, ind=True)
+                cp(A(wo, c0, c0 + nq), A("MB", 0, nq))
+                copy("KL", A("KL", c0, c0 + nq), A("MB", 8, 8 + nq))
+                copy("XV", A("XV", u0, u0 + nl), IND("Xt", 0, 4096, wo, c0, c0 + nq), True)
                 cq = (A("ones", 0, 128, p=1), A("QC", 0, nl, p=1))
                 ma, md = A("MA", 0, nl), A("MA", 256, 256 + nl)
                 xv = A("XV", u0, u0 + nl)
@@ -363,7 +379,10 @@ def build(g, core, T, topo):
                 ts(A("ZA", zo, zo + nl), ma, MAG, OP.add, -MAG, OP.add)
                 if s < 5:
                     zturn(b, A("ZA", zo, zo + nl))
-                act(A("GT", zo, zo + nl), md, AF.Sign)
+                if "GT" in ON_V:
+                    ts(A("GT", zo, zo + nl), md, 0.0, OP.is_gt, 2.0, OP.mult)
+                else:
+                    act(A("GT", zo, zo + nl), md, AF.Sign)
             if s in (4, 5):
                 a, m = (0, 64) if s == 4 else (64, 16)
                 for off, src in ((64, "GT"), (160, "ZA")):
@@ -477,30 +496,35 @@ def build(g, core, T, topo):
                 ts(A(bl, b, 16 * k, 2, p=LN[b]), A("ZR0", b, 16 * k, 2, p=LN[b]), A("thr", b, b + 1, p=LN[b]), OP.is_ge)
             tt(A(ex, 0, 128 * k), IND(bl, 0, 16 * k, "CEX", 0, 8 * k), A("MQ", 0, 128 * k), OP.mult, ind=True)
             for i, e in enumerate(es):
-                group([(A("ZR0", 512 + 16 * i, 527 + 16 * i), A("LG", 128 * x, 128 * x + 128),
-                        A(ex, 128 * i + 16 * x, 128 * i + 16 * x + 15)) for x in range(8)])
-            for i, e in enumerate(es):
-                c = 16 * e
-                tt(A("OT", c, c + 15), A("ZR0", 512 + 16 * i, 527 + 16 * i), A("D6", c, c + 15), OP.mult, two=False)
-                tt(A("OT2", c, c + 15), A("OT", c, c + 15), A("VP", c, c + 15), OP.max)
-                cp(A("OFF", c, c + 15), A("OT2", c, c + 15))
+                group([(A("ZR0", 512 + 16 * i, 528 + 16 * i), A("LG", 128 * x, 128 * x + 128),
+                        A(ex, 128 * i + 16 * x, 128 * i + 16 * x + 16)) for x in range(8)])
+            c, m = 16 * es[0], 16 * es[0] + 16 * k
+            tt(A("OT", c, m), A("ZR0", 512, 512 + 16 * k), A("D6", c, m), OP.mult, two=False)
+            tt(A("OT2", c, m), A("OT", c, m), A("VP", c, m), OP.max)
+            cp(A("OFF", c, m), A("OT2", c, m))
 
         def change(e):
             up = "UP%d" % (e % 2)
             tt(A(up), A("OH", 240 * e, 240 * e + 240), A("ZR1", 0, 240), OP.mult, two=False)
             lw = IND("Kt", 0, 4096, wo, 16 * e, 16 * e + 15)
             tt(A("T1"), lw, A(up), OP.mult, ind=True)
-            tt(A("KS"), lw, A("OHS", 240 * e, 240 * e + 240), OP.add, ind=True)
             ts(A("T2"), A("T1"), 5, OP.arith_shift_right)
-            tt(A("T3"), A("T2"), A("KS"), OP.add)
+            if KS_PE:
+                tt(A("KSF"), lw, A("OHS", 240 * e, 240 * e + 240), OP.add, ind=True)
+                ps_ = A("MA", 0, 240)
+                add("t", [lambda: PE.matmul(ps_[0], A("IDF")[0], A("KSF")[0], True, True)], [A("IDF"), A("KSF")], [ps_], 0.4)
+                tt(A("T3"), A("T2"), ps_, OP.add, two=False)
+            else:
+                tt(A("KS"), lw, A("OHS", 240 * e, 240 * e + 240), OP.add, ind=True)
+                tt(A("T3"), A("T2"), A("KS"), OP.add)
             ts(A("T4"), A("T3"), 4095, OP.bitwise_and)
             o = IND("Kt", 0, 4352, "OFF", 16 * e, 16 * e + 15)
             a = A("T4")
             add("v", [lambda: V.tensor_copy(o[0], a[0])], [a, (None, [o[1][1]], 0)], [(None, [o[1][0]], 0)], vcost(a, 1.0, True, True))
         lowest((4,), "BLW", "EXW")
-        lowest((3, 2), "BL", "EXB")
+        lowest((2, 3), "BL", "EXB")
         change(4)
-        lowest((1, 0), "BL", "EXB")
+        lowest((0, 1), "BL", "EXB")
         change(3)
         lowest((5,), "BLW", "EXW")
         change(2)
@@ -515,7 +539,7 @@ def build(g, core, T, topo):
             mm([(A("MA", 300, 301), A("ones", 0, 128), A("WRB"), True, True)])
             cp(A("WI"), A("MA", 300, 301))
             ts(A("WI2"), A("WI"), 1, OP.bitwise_and)
-            ts(A("THR1"), A("WI2"), 2.0, OP.mult, 6.0, OP.add)
+            ts(A("THR1"), A("WI2"), 2.0, OP.mult, T0, OP.add)
     group([(A("MA"), A("CI", 128 * a, 128 * a + 128), A("Xt", 512 * a, 512 * a + 512)) for a in range(8)])
     act(A("YX"), A("MA"), AF.Copy)
     dma("s", "ox", T.yx[:], T.YX[:], [A("YX")], [], 2.0)
@@ -534,7 +558,7 @@ def order(ops):
     for i, o in enumerate(ops):
         for d in o["deps"]:
             succ[d].append(i)
-    lat = 0.1
+    lat = 0.07
     prio = [0.0] * k
     for i in range(k - 1, -1, -1):
         prio[i] = ops[i]["cost"] + max([prio[j] + lat for j in succ[i]] or [0.0])
@@ -553,7 +577,7 @@ def order(ops):
                 continue
             f = free.get(q, 0.0)
             st = max(f, min(at[i] for i in c))
-            i = max((i for i in c if at[i] <= st + 1e-9), key=lambda i: prio[i] - 0.01 * i)
+            i = max((i for i in c if at[i] <= st + 1e-9), key=lambda i: prio[i] - ALPHA * i)
             if best is None or st < best[0]:
                 best = (st, q, i)
         st, q, i = best
@@ -563,7 +587,7 @@ def order(ops):
         end = st + o["cost"]
         done.append(i)
         for j in succ[i]:
-            at[j] = max(at[j], end + (lat if o["kind"] != "w" else 0.0))
+            at[j] = max(at[j], end + (lat if o["kind"] != "w" and (ops[j]["deps"][i] or o["kind"] != "c") else 0.0))
             left[j] -= 1
             if not left[j]:
                 pool.setdefault(ops[j]["q"], []).append(j)

@@ -10,8 +10,8 @@ ALPHA, KS_PE = 0.02, True
 ZBUF = (("ZR0", 0), ("ZR1", 0))
 CHUNKS = (((0, 32), (32, 64), (64, 96), (96, 128)), ((0, 32), (32, 64), (64, 96), (96, 112)))
 ON_S = ()
-ON_V = ("KL", "GT", "ZT")
-EQ_S = (0, 5)
+ON_V = ("GT", "ZT")
+EQ_S = (0, 15, 15, 15, 15, 0)
 BIG = 1048576.0
 MAG = 8388608.0
 MSG = 126
@@ -39,7 +39,9 @@ for _n, _c, _d in (
         ("LR", 2048, "bfloat16"), ("LS", 2048, "bfloat16"), ("ID", 128, "bfloat16"), ("HID", 128, "bfloat16"), ("RA", 256, "float16"),
         ("LG", 1024, "bfloat16"), ("LG16", 1024, "bfloat16"), ("M16", 16, "bfloat16"), ("BK", 16, "bfloat16"),
         ("KC", 256, "bfloat16"), ("QC", 240, "bfloat16"), ("C2K", 240, "bfloat16"), ("MSK", 256, "float32"),
-        ("MQ", 256, "bfloat16"), ("CEX", 16, "uint16"), ("gm", 8, "float32"), ("nkp", 1, "float32"),
+        ("MK", 640, "bfloat16"), ("MR", 128, "bfloat16"), ("EXK", 640, "bfloat16"), ("MK2", 160, "int32"), ("CEK", 40, "uint16"),
+        ("kj", 40, "float32"), ("kt", 40, "float32"), ("CE2", 16, "uint16"), ("i6", 192, "int32"), ("i7", 192, "int32"),
+        ("s0", 96, "float32"), ("s1", 96, "float32"), ("s2", 96, "float32"), ("CEX", 16, "uint16"), ("gm", 8, "float32"), ("nkp", 1, "float32"),
         ("pmf", 1, "float32"), ("CJ", 80, "float32"), ("CS", 80, "float32"), ("LANE", 16, "float32"),
         ("DUM", 80, "float32"), ("WT", 80, "float32"), ("thr", 3, "float32"), ("THR0", 1, "float32"),
         ("THR1", 1, "float32"), ("CI", 1024, "bfloat16"),
@@ -63,10 +65,10 @@ for _n, _c, _d in (
         ("T3", 240, "int32"), ("T4", 240, "int32"), ("KF", 4096, "float16"), ("YX", 512, "float32"), ("YK", 512, "float32"),
         ("WO0", 96, "uint16"), ("WO1", 96, "uint16"), ("ZC0", 240, "bfloat16"), ("ZC1", 240, "bfloat16"),
         ("PS0", 16, "float32"), ("PS1", 16, "float32"), ("RV0", 128, "float32"), ("RV1", 128, "float32"),
-        ("MI", 96, "int32"), ("F", 96, "int32"), ("BL", 64, "int32"), ("BLW", 32, "int32"), ("OT", 96, "float32"),
+        ("MI", 160, "int32"), ("F", 96, "int32"), ("BL", 64, "int32"), ("BLW", 32, "int32"), ("OT", 96, "float32"),
         ("OT2", 96, "float32"), ("OFF", 96, "uint16"), ("EXB", 256, "bfloat16"), ("EXW", 128, "bfloat16"),
         ("EQ", 6 * 3600, "bfloat16"), ("KVU", 240, "uint16"), ("KVH", 240, "float16"), ("KVC", 240, "float16"),
-        ("XG", 3840, "bfloat16"), ("RX", 3840, "bfloat16"), ("SC", 768, "float32"), ("EX", 576, "bfloat16"),
+        ("XG", 3840, "bfloat16"), ("RX", 3840, "bfloat16"), ("SC", 2560, "int32"), ("EX", 576, "bfloat16"),
         ("XV", 240, "bfloat16"), ("VRS", 240, "float32"), ("IDF", 128, "float32"), ("KSF", 240, "float32"), ("DF", 720, "float32"), ("NVM", 96, "float32"), ("ZT", 384, "bfloat16"), ("NID", 128, "bfloat16"), ("NHID", 128, "bfloat16")):
     _sb(_n, _c, _d)
 for _n, _c in (("ZR0", 1024), ("ZR1", 1024), ("KB0", 512), ("KB1", 512), ("MA", 512), ("MB", 512)):
@@ -211,7 +213,8 @@ def build(g, core, T, topo):
         dsts=[T.land[:, j * MSG:(j + 1) * MSG] for j in range(5)])], local_sem=T.sem["sent"])],
         [A("snd")], [], 1.0, sig=("sent", ne), kind="r")
     z_in = add("n", [], [], [], 6.0, kind="n")
-    ops[z_in]["deps"][z_in - 1] = True
+    z_out = z_in - 1
+    ops[z_in]["deps"][z_out] = True
     w = add("v", [lambda: V.wait_ge(T.sem["zarr"], 5 * ne)], [], [A("land")], 0.0, kind="w")
     ops[w]["deps"][z_in] = False
 
@@ -219,16 +222,24 @@ def build(g, core, T, topo):
         kw = {"allow_small_or_imprecise_dtypes": True} if flag else {}
         add("g", [lambda: g.iota(o[0], pattern, base, ch, **kw)], [], [o], 0.13 + 0.00166 * o[2])
 
-    def sel(o, a, pattern, base, ch):
-        add("g", [lambda: g.affine_select(o[0], a[0], pattern, OP.is_equal, 0.0, base, ch)], [a], [o], 0.17 + 0.00166 * o[2])
+    def sel(o, a, pattern, base, ch, op=OP.is_equal):
+        i = add("g", [lambda: g.affine_select(o[0], a[0], pattern, op, 0.0, base, ch)], [a], [o], 0.17 + 0.00166 * o[2])
+        if o[2] > 128:
+            ops[i]["deps"][z_out] = False
     ms(A("ones"), 1.0)
     sel(A("ID"), A("ones", 0, 128), [[-1, 128]], 0, 1)
     iota(A("pc"), [[0, 1]], 0, 1)
     iota(A("i0", 0, 16), [[-1, 16]], 128, 1)
     iota(A("i1", 0, 16), [[0, 2], [-16, 8]], 0, 1)
-    iota(A("i2"), [[0, 32], [-16, 8]], 0, 1)
     sel(A("E"), A("ones"), [[-1, 128], [0, 16]], 0, 1)
     iota(A("i3", 0, 16), [[16, 16]], 0, 0)
+    iota(A("i3", 16, 112), [[0, 6], [16, 16]], 4096, 0)
+    iota(A("i6", 0, 40), [[16, 40]], 0, 0)
+    iota(A("i6", 48, 64), [[0, 16]], 0, 0)
+    sel(A("MR"), A("ones", 0, 128), [[-16, 8], [0, 16]], 0, 1, OP.is_ge)
+    sel(A("MR"), A("MR"), [[16, 8], [0, 16]], 15, -1, OP.is_ge)
+    sel(A("MK"), A("ones", 0, 640), [[0, 80], [-16, 8]], 0, 1, OP.is_ge)
+    sel(A("MK"), A("MK"), [[0, 80], [16, 8]], 15, -1, OP.is_ge)
     iota(A("KC"), [[93 * 256, 2], [0, 8], [-256, 16]], 2560, 0, True)
     cp(A("IDF"), A("ID"))
     ts(A("HID"), A("ID"), 0.5, OP.mult, fast=True)
@@ -248,22 +259,26 @@ def build(g, core, T, topo):
     ts(A("i5"), A("i1", 0, 16), 4, OP.arith_shift_right)
     ts(A("BK"), A("i5"), 0.0, OP.is_equal, 4096.0, OP.mult)
     ts(A("gm"), A("i5", 0, 8), 0.0, OP.is_equal)
-    ts(A("i0"), A("i2"), 4, OP.arith_shift_right)
-    ts(A("MQ"), A("i0"), 0.0, OP.is_equal)
+
     ts(A("LANE"), A("i3", 0, 16), A("pmf"), OP.add)
     cp(A("i2", 0, 16), A("LANE"))
     ts(A("i1", 0, 16), A("i2", 0, 16), 3, OP.arith_shift_right)
-    cp(A("CEX"), A("i1", 0, 16))
-    for x in range(6):
-        ts(A("D6", 16 * x, 16 * x + 16), A("LANE"), 4096.0, OP.add)
+    cp(A("CE2"), A("i1", 0, 16))
+    ts(A("kj"), A("i6", 0, 40), A("pmf"), OP.add)
+    ts(A("i7", 0, 40), A("kj"), 1.0 / 80, OP.mult, -79.0 / 160, OP.add)
+    ts(A("kt"), A("i7", 0, 40), -80.0, OP.mult)
+    tt(A("i7", 64, 104), A("kj"), A("kt"), OP.add)
+    ts(A("i7", 128, 168), A("i7", 64, 104), 3, OP.arith_shift_right)
+    ts(A("kt"), A("i7", 128, 168), 16.0, OP.mult)
+    tt(A("kj"), A("kt"), A("i7", 0, 40), OP.add)
+    cp(A("CEK"), A("kj"))
+    ts(A("CEX"), A("i6", 48, 64), A("pmf"), OP.add)
+    ms(A("SC", 15, 2560, 16), 0)
+    ts(A("D6"), A("i3", 16, 112), A("pmf"), OP.add)
     ms(A("LG"), 0.0)
-    ms(A("LG16"), 0.0)
     for x in range(8):
         cp(A("LG", 144 * x, 144 * x + 16), A("M16"))
-        ts(A("LG16", 144 * x, 144 * x + 16), A("M16"), 16.0, OP.mult)
-    ms(A("LS"), 0.0)
-    for r in range(16):
-        cp(A("LS", 129 * r, 128 * r + 128, 16), A("gm"))
+    ts(A("LG16"), A("LG"), 16.0, OP.mult, fast=True)
     ms(A("F"), 0)
     ms(A("BL"), 0)
     ms(A("BLW"), 0)
@@ -274,6 +289,9 @@ def build(g, core, T, topo):
     ms(A("KL"), 0.0)
     ms(A("THR0"), T0)
     sel(A("LR"), A("ones"), [[-1, 16], [-16, 8], [0, 16]], 0, 1)
+    sel(A("LS"), A("ones"), [[-1, 16], [0, 8], [1, 16]], 0, 0)
+    sel(A("LS"), A("LS"), [[0, 16], [-16, 8], [0, 16]], 0, 1, OP.is_ge)
+    sel(A("LS"), A("LS"), [[0, 16], [16, 8], [0, 16]], 15, -1, OP.is_ge)
     for s in range(5):
         iota(A("cf", 16 * s, 16 * s + 15), [[1, 5], [0, 3]], 8 * (s + 1) + 1, 0, True)
     iota(A("cf", 96, 176), [[1, 5], [0, 16]], 1, 0, True)
@@ -292,12 +310,15 @@ def build(g, core, T, topo):
     tt(A("a7"), A("a7"), A("bf", 6, 7), OP.mult)
     for b in range(NB):
         ts(A("thr", b, b + 1), A("a7"), 2.0 ** (60 - 128 * b), OP.mult)
-    ms(A("cf", 176, 192), 0.0)
-    for c in range(15):
-        ms(A("cf", 176 + c, 177 + c), 2.0 ** (99 - 16 * c))
+    ms(A("s0"), 2.0 ** -16)
+    ms(A("s0", 0, 96, 16), 0.0)
+    ms(A("s0", 15, 96, 16), 0.0)
+    ms(A("s1"), 0.0)
+    ms(A("s1", 0, 96, 16), 2.0 ** 99)
+    add("v", [lambda: V.tensor_tensor_scan(A("s2")[0], A("s0")[0], A("s1")[0], 0.0, OP.mult, OP.add)],
+        [A("s0"), A("s1")], [A("s2")], 0.11)
     ts(A("a4"), A("a4"), 2.0 ** 20, OP.mult)
-    for x in range(6):
-        ts(A("W6", 16 * x, 16 * x + 16), A("cf", 176, 192), A("a4"), OP.mult)
+    ts(A("W6"), A("s2"), A("a4"), OP.mult)
     for e in range(6):
         for q in range(15):
             lo = 128 * (q // 8)
@@ -350,25 +371,19 @@ def build(g, core, T, topo):
                        (A(kb, 0, 256, p=nl), A("KVH", u0, u0 + nl), A("RA"))]
                 mm([x + (i == 0, False) for i, x in enumerate(lst)])
                 mm([(A(kb, k, 256, 16, p=nl), A("RX", 16 * u0 + k, 16 * (u0 + nl), 16), A("BK"), False, k == 15) for k in range(16)])
-                sc, mi, f, ex = 256 * b, 32 * b, 32 * b, 192 * b
+                sc, f, ex = 512 * (s - 1) + 256 * b, 32 * b, 192 * b
                 o = A("SC", sc, sc + 256, p=nl)
                 m_, kk = A("MSK", p=nl), A(kb, 0, 256, p=nl)
                 add("v", [lambda o=o, m_=m_, kk=kk: V.tensor_tensor_scan(o[0], m_[0], kk[0], 0.0, OP.mult, OP.max)],
                     [m_, kk], [o], vcost(o))
-                cp(A("MI", mi, mi + 16, p=nl), A("SC", sc + 15, sc + 256, 16, p=nl))
-                ts(A("F", f, f + 8, p=nl), A("MI", mi, mi + 8, p=nl), 255, OP.bitwise_and)
-                ts(A("F", f + 8, f + 24, 2, p=nl), A("MI", mi + 8, mi + 16, p=nl), 255, OP.bitwise_and)
-                ts(A("F", f + 9, f + 24, 2, p=nl), A("MI", mi, mi + 8, p=nl), 8, OP.arith_shift_right, 15, OP.bitwise_and)
-                tt(A("EX", ex, ex + 192), IND("F", f, f + 32, "CEX", 0, 12), A("MQ", 0, 192), OP.mult, ind=True)
+                ts(A("F", f, f + 16, p=nl), A("SC", sc + 15, sc + 256, 16, p=nl), 255, OP.bitwise_and)
+                tt(A("EX", ex, ex + 128), IND("F", f, f + 16, "CEX", 0, 8), A("MR"), OP.mult, ind=True)
                 lst = []
                 for x in range(8):
-                    e = ex + 64 + 16 * x
-                    lst.append((A("MB", 0, 16), A("LG", 128 * x, 128 * x + 128, p=nl), A("EX", e, e + 16, p=nl)))
-                    e = ex + 8 * x
-                    lst.append((A("MB", 0, 8), A("LG16", 128 * x, 128 * x + 128, p=nl), A("EX", e, e + 8, p=nl)))
+                    lst.append((A("MB", 0, 8), A("LG16", 128 * x, 128 * x + 128, p=nl), A("EX", ex + x, ex + 128, 16, p=nl)))
+                    lst.append((A("MB", 0, 8), A("LG", 128 * x, 128 * x + 128, p=nl), A("EX", ex + 8 + x, ex + 128, 16, p=nl)))
                 group(lst)
                 cp(A(wo, c0, c0 + nq), A("MB", 0, nq))
-                copy("KL", A("KL", c0, c0 + nq), A("MB", 8, 8 + nq))
                 copy("XV", A("XV", u0, u0 + nl), IND("Xt", 0, 4096, wo, c0, c0 + nq), True)
                 cq = (A("ones", 0, 128, p=1), A("QC", 0, nl, p=1))
                 ma, md = A("MA", 0, nl), A("MA", 256, 256 + nl)
@@ -391,6 +406,7 @@ def build(g, core, T, topo):
             if s == 4:
                 ts(A("VF16", 0, 80), A(wo, 0, 80), -2048.0, OP.add)
                 ts(A("VM", 0, 80), A(wo, 0, 80), -2048.0, OP.add)
+                ts(A("NVM", 0, 80), A("VM", 0, 80), -1.0, OP.mult)
         cp(A("WF"), A(wo))
         tt(A("TW"), A("WF", 16, 96), A("MB", 160, 240), OP.mult, two=False)
         ts(A("U"), A("TW"), 4095, OP.bitwise_and)
@@ -417,7 +433,7 @@ def build(g, core, T, topo):
         cp(A("WLU"), A("QW"))
         ts(A("VF16", 80, 96), A("QW"), -2048.0, OP.add)
         ts(A("VM", 80, 96), A("QW"), -2048.0, OP.add)
-        ts(A("NVM"), A("VM"), -1.0, OP.mult)
+        ts(A("NVM", 80, 96), A("VM", 80, 96), -1.0, OP.mult)
         ts(A("QZ"), A("QS"), 5.0, OP.min, 256.0, OP.mult)
         tt(A("QZ"), A("QZ"), A("LANE"), OP.add)
         ts(A("ZO"), A("QZ"), -256.0, OP.add)
@@ -427,16 +443,20 @@ def build(g, core, T, topo):
         def rows(out, src, a):
             mm([(A(out[0], out[1] + r, out[1] + 240, 16), A("LR", 128 * r, 128 * r + 128), A(src, a, a + 15), True, True)
                 for r in range(16)])
+        ts(A("MK2"), A("SC", 15, 2560, 16), 8, OP.arith_shift_right, 15, OP.bitwise_and)
+        tt(A("EXK"), IND("MK2", 0, 160, "CEK", 0, 40), A("MK"), OP.mult, ind=True)
+        group([(A("MB", 256, 336), A("LG", 128 * x, 128 * x + 128), A("EXK", 80 * x, 80 * x + 80)) for x in range(8)])
+        cp(A("KL", 16, 96), A("MB", 256, 336))
         for i, e in enumerate((4, 3, 2, 1, 0, 5)):
             rows(("KB0", 256), "VF16", 16 * e)
             vr = "VR%d" % (i % 2)
-            if e in EQ_S:
-                act(A("VRS"), A("KB0", 256, 496), AF.Copy)
-            else:
+            if EQ_S[e] < 15:
+                act(A("VRS", 16 * EQ_S[e], 240), A("KB0", 256 + 16 * EQ_S[e], 496), AF.Copy)
+            if EQ_S[e] > 0:
                 cp(A(vr), A("KB0", 256, 496))
             for q in range(15):
                 eq, col = A("EQ", e * 3600 + 256 * q, e * 3600 + 240 * q + 240), (16 * e + q, 16 * e + q + 1)
-                if e in EQ_S:
+                if q >= EQ_S[e]:
                     df = A("DF", 240 * (q % 3), 240 * (q % 3) + 240 - 16 * q)
                     act(df, A("VRS", 16 * q, 240), AF.Abs, bias=A("NVM", *col))
                     act(eq, df, AF.Relu, bias=1.0, scale=-1.0)
@@ -494,7 +514,7 @@ def build(g, core, T, topo):
             k = len(es)
             for b in range(NB):
                 ts(A(bl, b, 16 * k, 2, p=LN[b]), A("ZR0", b, 16 * k, 2, p=LN[b]), A("thr", b, b + 1, p=LN[b]), OP.is_ge)
-            tt(A(ex, 0, 128 * k), IND(bl, 0, 16 * k, "CEX", 0, 8 * k), A("MQ", 0, 128 * k), OP.mult, ind=True)
+            tt(A(ex, 0, 128 * k), IND(bl, 0, 16 * k, "CE2", 0, 8 * k), A("MK", 0, 128 * k), OP.mult, ind=True)
             for i, e in enumerate(es):
                 group([(A("ZR0", 512 + 16 * i, 528 + 16 * i), A("LG", 128 * x, 128 * x + 128),
                         A(ex, 128 * i + 16 * x, 128 * i + 16 * x + 16)) for x in range(8)])
@@ -562,6 +582,7 @@ def order(ops):
     prio = [0.0] * k
     for i in range(k - 1, -1, -1):
         prio[i] = ops[i]["cost"] + max([prio[j] + lat for j in succ[i]] or [0.0])
+    rank = [prio[i] - ALPHA * i for i in range(k)]
     left = [len(o["deps"]) for o in ops]
     at = [0.0] * k
     free = {}
@@ -577,7 +598,7 @@ def order(ops):
                 continue
             f = free.get(q, 0.0)
             st = max(f, min(at[i] for i in c))
-            i = max((i for i in c if at[i] <= st + 1e-9), key=lambda i: prio[i] - ALPHA * i)
+            i = max((i for i in c if at[i] <= st + 1e-9), key=lambda i: rank[i])
             if best is None or st < best[0]:
                 best = (st, q, i)
         st, q, i = best

import math
from concourse.bass import DstId, RemoteDMATransfer
from concourse.mybir import AluOpType, AxisListType, ActivationFunctionType

OP = AluOpType
AF = ActivationFunctionType
NB, LN = 2, (128, 112)
QB, QN = (0, 8), (8, 7)
ALPHA, KS_PE = 0.02, True
ZBUF = (("ZR0", 0), ("ZR1", 0))
CHUNKS = (((0, 32), (32, 64), (64, 96), (96, 128)), ((0, 32), (32, 64), (64, 96), (96, 112)))
ON_S = ()
ON_V = ("GT", "ZT")
EQ_S = (0, 15, 15, 15, 15, 0)
BIG = 1048576.0
MAG = 8388608.0
MSG = 126

SCRATCH = {}
VIEW = {}
PACK = {"float32": "pkf", "int32": "pki", "bfloat16": "pkb", "float16": "pkh", "uint16": "pku"}
OWN = ("zl", "vl", "snd", "land", "YX", "YK", "PS0", "PS1", "RV0", "RV1")


def _sb(name, cols, dtype, where="sbuf"):
    if where == "sbuf" and cols <= 512 and name not in OWN:
        pk = PACK[dtype]
        at = SCRATCH[pk][1][1] if pk in SCRATCH else 0
        SCRATCH[pk] = (where, [128, at + (cols + 31) // 32 * 32], dtype)
        VIEW[name] = (pk, at, cols)
    else:
        SCRATCH[name] = (where, [128, cols], dtype)
        VIEW[name] = (name, 0, cols)


for _n, _c, _d in (
        ("Xt", 4352, "bfloat16"), ("Kt", 4352, "int32"), ("zl", 96, "bfloat16"), ("vl", 30, "int32"),
        ("snd", MSG, "float16"), ("land", 5 * MSG, "float16"), ("ones", 2048, "bfloat16"), ("E", 2048, "bfloat16"),
        ("LR", 2048, "bfloat16"), ("LS", 2048, "bfloat16"), ("ID", 128, "bfloat16"), ("HID", 128, "bfloat16"), ("RA", 256, "float16"),
        ("LG", 1024, "bfloat16"), ("LG16", 1024, "bfloat16"), ("M16", 16, "bfloat16"), ("BK", 16, "bfloat16"),
        ("KC", 256, "bfloat16"), ("QC", 240, "bfloat16"), ("C2K", 240, "bfloat16"), ("MSK", 256, "float32"),
        ("MK", 640, "bfloat16"), ("MR", 128, "bfloat16"), ("EXK", 640, "bfloat16"), ("MK2", 160, "int32"), ("CEK", 40, "uint16"),
        ("kj", 40, "float32"), ("kt", 40, "float32"), ("CE2", 16, "uint16"), ("i6", 192, "int32"), ("i7", 192, "int32"),
        ("s0", 96, "float32"), ("s1", 96, "float32"), ("s2", 96, "float32"), ("CEX", 16, "uint16"), ("gm", 8, "float32"), ("nkp", 1, "float32"),
        ("pmf", 1, "float32"), ("CJ", 80, "float32"), ("CS", 80, "float32"), ("LANE", 16, "float32"),
        ("DUM", 80, "float32"), ("WT", 80, "float32"), ("thr", 3, "float32"), ("THR0", 1, "float32"),
        ("THR1", 1, "float32"), ("CI", 1024, "bfloat16"),
        ("i0", 256, "int32"), ("i1", 256, "int32"), ("i2", 256, "int32"), ("i3", 256, "int32"), ("i4", 16, "int32"), ("i5", 16, "int32"),
        ("pc", 1, "int32"), ("pm", 1, "int32"), ("bits", 8, "int32"), ("bf", 8, "float32"), ("a4", 1, "float32"),
        ("a7", 1, "float32"), ("cf", 256, "float32"),
        ("ZA", 1280, "bfloat16"), ("GT", 1280, "bfloat16"), ("KL", 96, "bfloat16"),
        ("VF16", 96, "float16"), ("WF", 96, "float32"), ("VM", 96, "float32"),
        ("TW", 80, "int32"), ("U", 80, "int32"), ("PEN", 80, "float32"), ("P1", 80, "float32"), ("P2", 80, "float32"),
        ("P3", 32, "float32"), ("P4", 16, "float32"), ("Q1", 80, "float32"), ("Q2", 80, "float32"), ("Q3", 32, "float32"),
        ("Q4", 16, "float32"), ("Q5", 16, "int32"), ("QW", 16, "int32"), ("QS", 16, "int32"), ("QZ", 16, "float32"),
        ("ZO", 16, "uint16"), ("WLU", 16, "uint16"), ("WL", 16, "float32"), ("WL16", 16, "float16"), ("WLM", 16, "float32"),
        ("BA", 16, "float32"), ("BB", 16, "float32"), ("BC", 16, "float32"), ("BI", 16, "int32"), ("END", 16, "int32"),
        ("UW", 16, "int32"), ("U16", 16, "float16"), ("W1", 16, "float32"), ("NBD", 16, "float32"), ("WON", 16, "float32"),
        ("L1", 16, "float32"), ("LE", 16, "float32"), ("CN6", 96, "float32"), ("NC6", 96, "float32"), ("ND6", 96, "float32"),
        ("VP", 96, "float32"), ("CW6", 96, "float32"), ("CM", 768, "bfloat16"), ("WR", 1, "float32"), ("WRB", 1, "bfloat16"),
        ("WI", 1, "int32"), ("WI2", 1, "int32"), ("W6", 96, "float32"), ("D6", 96, "float32"),
        ("OH", 1200, "bfloat16"), ("OHS", 1200, "bfloat16"), ("AB0", 240, "float32"), ("AB1", 240, "float32"),
        ("VR0", 240, "float16"), ("VR1", 240, "float16"), ("XW", 240, "bfloat16"), ("ZS", 240, "bfloat16"),
        ("NX", 240, "bfloat16"), ("UP0", 240, "float32"), ("UP1", 240, "float32"), ("T1", 240, "int32"), ("KS", 240, "int32"), ("T2", 240, "int32"),
        ("T3", 240, "int32"), ("T4", 240, "int32"), ("KF", 4096, "float16"), ("YX", 512, "float32"), ("YK", 512, "float32"),
        ("WO0", 96, "uint16"), ("WO1", 96, "uint16"), ("ZC0", 240, "bfloat16"), ("ZC1", 240, "bfloat16"),
        ("PS0", 16, "float32"), ("PS1", 16, "float32"), ("RV0", 128, "float32"), ("RV1", 128, "float32"),
        ("MI", 160, "int32"), ("F", 96, "int32"), ("BL", 64, "int32"), ("BLW", 32, "int32"), ("OT", 96, "float32"),
        ("OT2", 96, "float32"), ("OFF", 96, "uint16"), ("EXB", 256, "bfloat16"), ("EXW", 128, "bfloat16"),
        ("EQ", 6 * 3600, "bfloat16"), ("KVU", 240, "uint16"), ("KVH", 240, "float16"), ("KVC", 240, "float16"),
        ("XG", 3840, "bfloat16"), ("RX", 3840, "bfloat16"), ("SC", 2560, "int32"), ("EX", 576, "bfloat16"),
        ("XV", 240, "bfloat16"), ("VRS", 240, "float32"), ("IDF", 128, "float32"), ("KSF", 240, "float32"), ("DF", 720, "float32"), ("NVM", 96, "float32"), ("ZT", 384, "bfloat16"), ("NID", 128, "bfloat16"), ("NHID", 128, "bfloat16")):
    _sb(_n, _c, _d)
for _n, _c in (("ZR0", 1024), ("ZR1", 1024), ("KB0", 512), ("KB1", 512), ("MA", 512), ("MB", 512)):
    _sb(_n, _c, "float32", "psum")
QS = ("v", "s", "t", "g")
DMAS = ("dz", "dv", "dk", "dx", "ox", "ok")
SEMAPHORES = ["qv", "qs", "qt", "qg"] + list(DMAS) + ["zarr", "parr0", "parr1", "sent"]


def build(g, core, T, topo):
    rank = T.rank_of(core)
    n = len(T.cores)
    ops = []
    hist = {}

    def A(name, a=0, b=None, st=1, p=128, p0=0):
        home, at, cols = VIEW[name]
        buf = T[home]
        b = cols if b is None else b
        if SCRATCH[home][0] == "psum":
            reg = [("%s.%d" % (name, k), 0, 1, 1, True) for k in range(a // 512, (b - 1) // 512 + 1)]
        else:
            reg = [(name, a, b, st, False)]
        ap = buf[p0:p, at + a:at + b] if st == 1 else buf[p0:p, at + a:at + b:st]
        return ap, reg, len(range(a, b, st))

    def IND(win, a, b, off, c, d):
        return A(win, a, b)[0].indirect(A(off, c, d)[0]), [(win, a, b, 1, False), (off, c, d, 1, False)], 16 * (d - c)

    def add(q, calls, reads, writes, cost, sig=None, kind="c"):
        i = len(ops)
        deps = {}
        for acc, wr in ((reads, False), (writes, True)):
            for x in acc:
                for (name, a, b, st, ps) in x[1]:
                    for (a2, b2, s2, w2, q2, j) in hist.get(name, ()):
                        if j == i:
                            continue
                        if ps:
                            if q2 != q:
                                deps[j] = True
                            else:
                                deps.setdefault(j, False)
                            continue
                        if not (wr or w2) or a >= b2 or a2 >= b:
                            continue
                        if st == s2 and st > 1 and (a - a2) % st:
                            continue
                        if q2 == q == "t":
                            deps.setdefault(j, False)
                        else:
                            deps[j] = True
        for acc, wr in ((reads, False), (writes, True)):
            for x in acc:
                for (name, a, b, st, ps) in x[1]:
                    h = hist.setdefault(name, set())
                    if ps:
                        h -= {k for k in h if k[4] != q}
                    elif wr and st == 1:
                        h -= {k for k in h if k[0] >= a and k[1] <= b and k[5] != i}
                    h.add((a, b, st, wr, q if kind == "c" else "%s%d" % (q, i), i))
        ops.append({"q": q, "calls": calls, "deps": deps, "cost": cost, "sig": sig, "kind": kind,
                    "name": writes[0][1][0][0] if writes else ""})
        return i

    V, S, PE = g.vector, g.scalar, g.tensor
    T0 = 22.0 if "GT" in ON_V else 6.0

    def vcost(o, per=1.0, ind=False, sc=False):
        return (0.03 if not ind else 0.05) + (1.56 if ind and not sc else 3.5 if sc else per) * max(o[2], 1 if ind else 64) * 0.00083

    def cp(o, a, ind=False, sc=False, fast=False):
        add("v", [lambda: V.tensor_copy(o[0], a[0])], [a], [o], vcost(a if sc else o, 0.5 if fast else 1.0, ind, sc))

    def tt(o, a, b, op, ind=False, two=True):
        add("v", [lambda: V.tensor_tensor(o[0], a[0], b[0], op)], [a, b], [o], vcost(o, 2.0 if two else 1.0, ind))

    def ts(o, a, s1, op0, s2=None, op1=None, fast=False):
        r = [a] + [x for x in (s1, s2) if isinstance(x, tuple)]
        v1 = s1[0] if isinstance(s1, tuple) else s1
        v2 = s2[0] if isinstance(s2, tuple) else s2
        if op1 is None:
            c = lambda: V.tensor_scalar(o[0], a[0], v1, None, op0)
        else:
            c = lambda: V.tensor_scalar(o[0], a[0], v1, v2, op0, op1)
        add("v", [c], r, [o], vcost(o, 0.5 if fast else 1.0))

    def ms(o, val):
        add("v", [lambda: V.memset(o[0], val)], [], [o], vcost(o, 0.5))

    def act(o, a, func, bias=None, scale=None, ind=False):
        r = [a] + [x for x in (bias, scale) if isinstance(x, tuple)]
        kw = {}
        if bias is not None:
            kw["bias"] = bias[0] if isinstance(bias, tuple) else bias
        if scale is not None:
            kw["scale"] = scale[0] if isinstance(scale, tuple) else scale
        add("s", [lambda: S.activation(o[0], a[0], func, **kw)], r, [o], 0.05 + (1.56 if ind else 1.0) * o[2] * 0.00083)

    def copy(what, o, a, ind=False):
        if what in ON_V:
            cp(o, a, ind=ind)
        else:
            act(o, a, AF.Copy, ind=ind)

    def mm(lst):
        def one(x):
            return lambda: PE.matmul(x[0][0], x[1][0], x[2][0], x[3], x[4])
        add("t", [one(x) for x in lst], [y for x in lst for y in (x[1], x[2])], [x[0] for x in lst],
            sum(max(64, x[0][2]) for x in lst) * 0.000417)

    def group(lst):
        k = len(lst)
        mm([(o, a, b, i == 0, i == k - 1) for i, (o, a, b) in enumerate(lst)])

    def dma(q, sem, out, in_, reads, writes, lat):
        eng = g.sync if q == "y" else g.scalar
        add(q, [lambda: eng.dma_start(out, in_).then_inc(T.sem[sem], 16)], reads, writes, lat, sig=(sem, 16), kind="d")

    dma("y", "dz", T.zl[:], T.z0[:], [], [A("zl")], 2.0)
    dma("s", "dv", T.vl[:], T.v0[:], [], [A("vl")], 2.0)
    dma("y", "dk", T.Kt[:, 0:4096], T.k0[:], [], [A("Kt", 0, 4096)], 8.0)
    dma("s", "dx", T.Xt[:, 0:4096], T.x0[:], [], [A("Xt", 0, 4096)], 8.0)
    cp(A("snd", 0, 96), A("zl"), fast=True)
    ts(A("snd", 96, MSG), A("vl"), -2048.0, OP.add)
    hosts = [T.cores[(rank + j) % n] for j in range(1, 6)]
    peers = [T.cores[(rank + d) % n] for d in range(1, n)]

    def dest(c):
        a = topo.addr(c)
        return DstId(rid=a[0], pnc=a[1])

    def common(lst):
        m = topo.mask(core, lst[0])
        for c in lst:
            m &= topo.mask(core, c)
        return m
    mk = common(peers)
    ne = bin(mk).count("1")
    add("g", [lambda: g.remote_dma_fused([RemoteDMATransfer(
        dst_ids=[dest(c) for c in hosts], dma_engine_mask=mk, remote_sem=T.sem["zarr"], srcs=[T.snd[:]],
        dsts=[T.land[:, j * MSG:(j + 1) * MSG] for j in range(5)])], local_sem=T.sem["sent"])],
        [A("snd")], [], 1.0, sig=("sent", ne), kind="r")
    z_in = add("n", [], [], [], 6.0, kind="n")
    z_out = z_in - 1
    ops[z_in]["deps"][z_out] = True
    w = add("v", [lambda: V.wait_ge(T.sem["zarr"], 5 * ne)], [], [A("land")], 0.0, kind="w")
    ops[w]["deps"][z_in] = False

    def iota(o, pattern, base, ch, flag=False):
        kw = {"allow_small_or_imprecise_dtypes": True} if flag else {}
        add("g", [lambda: g.iota(o[0], pattern, base, ch, **kw)], [], [o], 0.13 + 0.00166 * o[2])

    def sel(o, a, pattern, base, ch, op=OP.is_equal):
        i = add("g", [lambda: g.affine_select(o[0], a[0], pattern, op, 0.0, base, ch)], [a], [o], 0.17 + 0.00166 * o[2])
        if o[2] > 128:
            ops[i]["deps"][z_out] = False
    ms(A("ones"), 1.0)
    sel(A("ID"), A("ones", 0, 128), [[-1, 128]], 0, 1)
    iota(A("pc"), [[0, 1]], 0, 1)
    iota(A("i0", 0, 16), [[-1, 16]], 128, 1)
    iota(A("i1", 0, 16), [[0, 2], [-16, 8]], 0, 1)
    sel(A("E"), A("ones"), [[-1, 128], [0, 16]], 0, 1)
    iota(A("i3", 0, 16), [[16, 16]], 0, 0)
    iota(A("i3", 16, 112), [[0, 6], [16, 16]], 4096, 0)
    iota(A("i6", 0, 40), [[16, 40]], 0, 0)
    iota(A("i6", 48, 64), [[0, 16]], 0, 0)
    sel(A("MR"), A("ones", 0, 128), [[-16, 8], [0, 16]], 0, 1, OP.is_ge)
    sel(A("MR"), A("MR"), [[16, 8], [0, 16]], 15, -1, OP.is_ge)
    sel(A("MK"), A("ones", 0, 640), [[0, 80], [-16, 8]], 0, 1, OP.is_ge)
    sel(A("MK"), A("MK"), [[0, 80], [16, 8]], 15, -1, OP.is_ge)
    iota(A("KC"), [[93 * 256, 2], [0, 8], [-256, 16]], 2560, 0, True)
    cp(A("IDF"), A("ID"))
    ts(A("HID"), A("ID"), 0.5, OP.mult, fast=True)
    ts(A("NHID"), A("ID"), -0.5, OP.mult, fast=True)
    ts(A("NID"), A("ID"), -1.0, OP.mult, fast=True)
    cp(A("RA", 0, 128), A("ID"), fast=True)
    ts(A("RA", 128, 256), A("ID"), -16.0, OP.mult, fast=True)
    ms(A("QC"), -0.25)
    ms(A("C2K"), 2048.0)
    ms(A("MSK"), 1.0)
    ms(A("MSK", 0, 256, 16), 0.0)
    ts(A("pm"), A("pc"), 15, OP.bitwise_and)
    cp(A("pmf"), A("pm"))
    ts(A("nkp"), A("pmf"), -15.0, OP.add)
    ts(A("i4"), A("i0", 0, 16), 15, OP.bitwise_and)
    ts(A("M16"), A("i4"), 0.0, OP.is_equal)
    ts(A("i5"), A("i1", 0, 16), 4, OP.arith_shift_right)
    ts(A("BK"), A("i5"), 0.0, OP.is_equal, 4096.0, OP.mult)
    ts(A("gm"), A("i5", 0, 8), 0.0, OP.is_equal)

    ts(A("LANE"), A("i3", 0, 16), A("pmf"), OP.add)
    cp(A("i2", 0, 16), A("LANE"))
    ts(A("i1", 0, 16), A("i2", 0, 16), 3, OP.arith_shift_right)
    cp(A("CE2"), A("i1", 0, 16))
    ts(A("kj"), A("i6", 0, 40), A("pmf"), OP.add)
    ts(A("i7", 0, 40), A("kj"), 1.0 / 80, OP.mult, -79.0 / 160, OP.add)
    ts(A("kt"), A("i7", 0, 40), -80.0, OP.mult)
    tt(A("i7", 64, 104), A("kj"), A("kt"), OP.add)
    ts(A("i7", 128, 168), A("i7", 64, 104), 3, OP.arith_shift_right)
    ts(A("kt"), A("i7", 128, 168), 16.0, OP.mult)
    tt(A("kj"), A("kt"), A("i7", 0, 40), OP.add)
    cp(A("CEK"), A("kj"))
    ts(A("CEX"), A("i6", 48, 64), A("pmf"), OP.add)
    ms(A("SC", 15, 2560, 16), 0)
    ts(A("D6"), A("i3", 16, 112), A("pmf"), OP.add)
    ms(A("LG"), 0.0)
    for x in range(8):
        cp(A("LG", 144 * x, 144 * x + 16), A("M16"))
    ts(A("LG16"), A("LG"), 16.0, OP.mult, fast=True)
    ms(A("F"), 0)
    ms(A("BL"), 0)
    ms(A("BLW"), 0)
    ms(A("WO0"), 0)
    ms(A("WO1"), 0)
    ms(A("GT"), 0.0)
    ms(A("ZA"), 0.0)
    ms(A("KL"), 0.0)
    ms(A("THR0"), T0)
    sel(A("LR"), A("ones"), [[-1, 16], [-16, 8], [0, 16]], 0, 1)
    sel(A("LS"), A("ones"), [[-1, 16], [0, 8], [1, 16]], 0, 0)
    sel(A("LS"), A("LS"), [[0, 16], [-16, 8], [0, 16]], 0, 1, OP.is_ge)
    sel(A("LS"), A("LS"), [[0, 16], [16, 8], [0, 16]], 15, -1, OP.is_ge)
    for s in range(5):
        iota(A("cf", 16 * s, 16 * s + 15), [[1, 5], [0, 3]], 8 * (s + 1) + 1, 0, True)
    iota(A("cf", 96, 176), [[1, 5], [0, 16]], 1, 0, True)
    ms(A("CJ"), 0.0)
    for s in range(5):
        ts(A("CJ", 16 * s, 16 * s + 15), A("cf", 16 * s, 16 * s + 15), 4096.0, OP.mult)
    ts(A("CS"), A("cf", 96, 176), 4096.0, OP.mult)
    for i in range(7):
        ts(A("bits", i, i + 1), A("pc"), i, OP.arith_shift_right, 1, OP.bitwise_and)
        ts(A("bf", i, i + 1), A("bits", i, i + 1), 0.0, OP.is_equal, 2.0 ** -(1 << i), OP.max)
    tt(A("a4"), A("bf", 0, 1), A("bf", 1, 2), OP.mult)
    tt(A("a4"), A("a4"), A("bf", 2, 3), OP.mult)
    tt(A("a4"), A("a4"), A("bf", 3, 4), OP.mult)
    ts(A("a7"), A("a4"), 2.0 ** 60, OP.mult, A("bf", 4, 5), OP.mult)
    tt(A("a7"), A("a7"), A("bf", 5, 6), OP.mult)
    tt(A("a7"), A("a7"), A("bf", 6, 7), OP.mult)
    for b in range(NB):
        ts(A("thr", b, b + 1), A("a7"), 2.0 ** (60 - 128 * b), OP.mult)
    ms(A("s0"), 2.0 ** -16)
    ms(A("s0", 0, 96, 16), 0.0)
    ms(A("s0", 15, 96, 16), 0.0)
    ms(A("s1"), 0.0)
    ms(A("s1", 0, 96, 16), 2.0 ** 99)
    add("v", [lambda: V.tensor_tensor_scan(A("s2")[0], A("s0")[0], A("s1")[0], 0.0, OP.mult, OP.add)],
        [A("s0"), A("s1")], [A("s2")], 0.11)
    ts(A("a4"), A("a4"), 2.0 ** 20, OP.mult)
    ts(A("W6"), A("s2"), A("a4"), OP.mult)
    for e in range(6):
        for q in range(15):
            lo = 128 * (q // 8)
            if 16 * q > lo:
                iota(A("EQ", e * 3600 + 240 * q + lo, e * 3600 + 256 * q), [[0, 16 * q - lo]], 0, 0, True)
    for a in range(8):
        ts(A("CI", 128 * a, 128 * a + 128), A("ID"), float(a + 1), OP.mult, fast=True)

    for t in range(2):
        wo, zc, ps, rv, par = "WO%d" % t, "ZC%d" % t, "PS%d" % t, "RV%d" % t, "parr%d" % t
        for j in range(5):
            o = j * MSG
            ts(A(wo, 3 * j, 3 * j + 3), A("land", o + 96 + t * 15 + 3 * j, o + 99 + t * 15 + 3 * j), 2048.0, OP.add)
            cp(A(zc, 48 * j, 48 * j + 48), A("land", o + t * 48, o + t * 48 + 48), fast=True)

        def zturn(b, z):
            m = 16 * QN[b]
            mm([(A("MA", 128, 256, p=m), z, A("ID"), True, True)])
            copy("ZT", A("ZT", 128 * b, 128 * b + 128, p=m), A("MA", 128, 256, p=m))
        for b in range(len(QB)):
            zturn(b, A(zc, 16 * QB[b], 16 * (QB[b] + QN[b])))
        nb, nch = 0, 0
        for s in range(1, 6):
            for b in range(len(QB)):
                nl, nq = 16 * QN[b], QN[b]
                l0, c0, u0 = (s - 1) * 16 + QB[b], s * 16 + QB[b], 16 * QB[b]
                kb = "KB%d" % (nb % 2)
                nb += 1
                z = A(zc, u0, u0 + nl) if s == 1 else A("ZA", (s - 2) * 256 + u0, (s - 2) * 256 + u0 + nl)
                cp(A("KVU", u0, u0 + nl), IND("Kt", 0, 4096, wo, l0, l0 + nq), ind=True)
                zt = A("ZT", 128 * b, 128 * b + 128, p=nl)
                for h, (a, e) in enumerate(CHUNKS[b]):
                    x0, x1 = 16 * (u0 + a), 16 * (u0 + e)
                    zr, z0, w = ZBUF[nch % len(ZBUF)] + (16 * (e - a),)
                    nch += 1
                    copy(("XG", b, h), A("XG", x0, x1), IND("Xt", 0, 4096, "KVU", u0 + a, u0 + e), True)
                    cuts = [(k, min(k + 512, w)) for k in range(0, w, 512)]
                    if (b, h) in ON_S:
                        for k, m in cuts:
                            zk = A(zr, z0 + k, z0 + m)
                            group([(zk, zt, A("E", 16 * a + k, 16 * a + m, p=nl)), (zk, A("NID"), A("XG", x0 + k, x0 + m))])
                        act(A("RX", x0, x1), A(zr, z0, z0 + w), AF.Relu, scale=-1.0)
                    else:
                        mm([(A(zr, z0 + k, z0 + m), zt, A("E", 16 * a + k, 16 * a + m, p=nl), True, True) for k, m in cuts])
                        tt(A("RX", x0, x1), A("XG", x0, x1), A(zr, z0, z0 + w), OP.max, two=False)
                ts(A("KVH", u0, u0 + nl), A("KVU", u0, u0 + nl), 1.0 / 16, OP.mult, 1280.0 - 15.0 / 32, OP.add, fast=True)
                ts(A("KVC", u0, u0 + nl), A("KVU", u0, u0 + nl), -2048.0, OP.add, fast=True)
                lst = [(A(kb, 0, 256, p=nl), A("ones", 0, nl, p=1), A("KC", p=1)),
                       (A(kb, 128, 256, p=nl), A("KVC", u0, u0 + nl), A("RA", 0, 128)),
                       (A(kb, 0, 256, p=nl), A("KVH", u0, u0 + nl), A("RA"))]
                mm([x + (i == 0, False) for i, x in enumerate(lst)])
                mm([(A(kb, k, 256, 16, p=nl), A("RX", 16 * u0 + k, 16 * (u0 + nl), 16), A("BK"), False, k == 15) for k in range(16)])
                sc, f, ex = 512 * (s - 1) + 256 * b, 32 * b, 192 * b
                o = A("SC", sc, sc + 256, p=nl)
                m_, kk = A("MSK", p=nl), A(kb, 0, 256, p=nl)
                add("v", [lambda o=o, m_=m_, kk=kk: V.tensor_tensor_scan(o[0], m_[0], kk[0], 0.0, OP.mult, OP.max)],
                    [m_, kk], [o], vcost(o))
                ts(A("F", f, f + 16, p=nl), A("SC", sc + 15, sc + 256, 16, p=nl), 255, OP.bitwise_and)
                tt(A("EX", ex, ex + 128), IND("F", f, f + 16, "CEX", 0, 8), A("MR"), OP.mult, ind=True)
                lst = []
                for x in range(8):
                    lst.append((A("MB", 0, 8), A("LG16", 128 * x, 128 * x + 128, p=nl), A("EX", ex + x, ex + 128, 16, p=nl)))
                    lst.append((A("MB", 0, 8), A("LG", 128 * x, 128 * x + 128, p=nl), A("EX", ex + 8 + x, ex + 128, 16, p=nl)))
                group(lst)
                cp(A(wo, c0, c0 + nq), A("MB", 0, nq))
                copy("XV", A("XV", u0, u0 + nl), IND("Xt", 0, 4096, wo, c0, c0 + nq), True)
                cq = (A("ones", 0, 128, p=1), A("QC", 0, nl, p=1))
                ma, md = A("MA", 0, nl), A("MA", 256, 256 + nl)
                xv = A("XV", u0, u0 + nl)
                group([(ma, cq[0], cq[1]), (ma, A("HID"), z), (ma, A("HID"), xv)])
                group([(md, cq[0], cq[1]), (md, A("NHID"), z), (md, A("HID"), xv)])
                zo = (s - 1) * 256 + u0
                ts(A("ZA", zo, zo + nl), ma, MAG, OP.add, -MAG, OP.add)
                if s < 5:
                    zturn(b, A("ZA", zo, zo + nl))
                if "GT" in ON_V:
                    ts(A("GT", zo, zo + nl), md, 0.0, OP.is_gt, 2.0, OP.mult)
                else:
                    act(A("GT", zo, zo + nl), md, AF.Sign)
            if s in (4, 5):
                a, m = (0, 64) if s == 4 else (64, 16)
                for off, src in ((64, "GT"), (160, "ZA")):
                    group([(A("MB", off + a, off + a + m), A("LS", 128 * r, 128 * r + 128),
                            A(src, 16 * a + r, 16 * (a + m), 16)) for r in range(16)])
            if s == 4:
                ts(A("VF16", 0, 80), A(wo, 0, 80), -2048.0, OP.add)
                ts(A("VM", 0, 80), A(wo, 0, 80), -2048.0, OP.add)
                ts(A("NVM", 0, 80), A("VM", 0, 80), -1.0, OP.mult)
        cp(A("WF"), A(wo))
        tt(A("TW"), A("WF", 16, 96), A("MB", 160, 240), OP.mult, two=False)
        ts(A("U"), A("TW"), 4095, OP.bitwise_and)
        ts(A("PEN"), A("MB", 64, 144), A("THR%d" % t), OP.is_lt, BIG, OP.mult)
        tt(A("P1"), A("U"), A("CJ"), OP.add)
        tt(A("P2"), A("P1"), A("PEN"), OP.add)
        tt(A("P3"), A("P2", 0, 32), A("P2", 32, 64), OP.min)
        tt(A("P4"), A("P3", 0, 16), A("P3", 16, 32), OP.min)
        tt(A(ps), A("P4"), A("P2", 64, 80), OP.min)
        add("g", [lambda ps=ps, rv=rv, par=par: g.remote_dma_fused([RemoteDMATransfer(
            dst_ids=[dest(c) for c in peers], dma_engine_mask=mk, remote_sem=T.sem[par], srcs=[T[ps][:]],
            dsts=[T[rv][:, 16 * rank:16 * rank + 16] for c in peers])], local_sem=T.sem["sent"])],
            [A(ps)], [], 1.0, sig=("sent", ne * (t + 2)), kind="r")
        p_in = add("n", [], [], [], 5.0, kind="n")
        ops[p_in]["deps"][p_in - 1] = True
        tt(A("Q1"), A("WF", 16, 96), A("CS"), OP.add)
        tt(A("Q2"), A("Q1"), A("PEN"), OP.add)
        tt(A("Q3"), A("Q2", 0, 32), A("Q2", 32, 64), OP.min)
        tt(A("Q4"), A("Q3", 0, 16), A("Q3", 16, 32), OP.min)
        tt(A("Q5"), A("Q4"), A("Q2", 64, 80), OP.min)
        ts(A("QW"), A("Q5"), 4095, OP.bitwise_and)
        ts(A("QS"), A("Q5"), 12, OP.arith_shift_right)
        cp(A("WF", 80, 96), A("QW"))
        cp(A("WLU"), A("QW"))
        ts(A("VF16", 80, 96), A("QW"), -2048.0, OP.add)
        ts(A("VM", 80, 96), A("QW"), -2048.0, OP.add)
        ts(A("NVM", 80, 96), A("VM", 80, 96), -1.0, OP.mult)
        ts(A("QZ"), A("QS"), 5.0, OP.min, 256.0, OP.mult)
        tt(A("QZ"), A("QZ"), A("LANE"), OP.add)
        ts(A("ZO"), A("QZ"), -256.0, OP.add)
        act(A("XW"), IND("Xt", 0, 4096, "WLU", 0, 15), AF.Copy, ind=True)
        act(A("ZS"), IND("ZA", 0, 1280, "ZO", 0, 15), AF.Copy, ind=True)

        def rows(out, src, a):
            mm([(A(out[0], out[1] + r, out[1] + 240, 16), A("LR", 128 * r, 128 * r + 128), A(src, a, a + 15), True, True)
                for r in range(16)])
        ts(A("MK2"), A("SC", 15, 2560, 16), 8, OP.arith_shift_right, 15, OP.bitwise_and)
        tt(A("EXK"), IND("MK2", 0, 160, "CEK", 0, 40), A("MK"), OP.mult, ind=True)
        group([(A("MB", 256, 336), A("LG", 128 * x, 128 * x + 128), A("EXK", 80 * x, 80 * x + 80)) for x in range(8)])
        cp(A("KL", 16, 96), A("MB", 256, 336))
        for i, e in enumerate((4, 3, 2, 1, 0, 5)):
            rows(("KB0", 256), "VF16", 16 * e)
            vr = "VR%d" % (i % 2)
            if EQ_S[e] < 15:
                act(A("VRS", 16 * EQ_S[e], 240), A("KB0", 256 + 16 * EQ_S[e], 496), AF.Copy)
            if EQ_S[e] > 0:
                cp(A(vr), A("KB0", 256, 496))
            for q in range(15):
                eq, col = A("EQ", e * 3600 + 256 * q, e * 3600 + 240 * q + 240), (16 * e + q, 16 * e + q + 1)
                if q >= EQ_S[e]:
                    df = A("DF", 240 * (q % 3), 240 * (q % 3) + 240 - 16 * q)
                    act(df, A("VRS", 16 * q, 240), AF.Abs, bias=A("NVM", *col))
                    act(eq, df, AF.Relu, bias=1.0, scale=-1.0)
                else:
                    ts(eq, A(vr, 16 * q, 240), A("VM", *col), OP.is_equal, fast=True)
            if e < 5:
                s = e + 1
                rows(("KB1", 256), "KL", 16 * s)
                ab = "AB%d" % (i % 2)
                act(A(ab), A("KB1", 256, 496), AF.Abs, bias=A("nkp"))
                act(A("OH", 240 * e, 240 * e + 240), A(ab), AF.Relu, bias=1.0, scale=-1.0)
                act(A("OHS", 240 * e, 240 * e + 240), A(ab), AF.Relu, bias=float(s), scale=-float(s))
        group([(A("ZR1", 512, 752), A("ones", 0, 128, p=1), A("QC", p=1)), (A("ZR1", 512, 752), A("HID"), A("XW")),
               (A("ZR1", 512, 752), A("HID"), A("ZS"))])
        ts(A("NX"), A("ZR1", 512, 752), MAG, OP.add, -MAG, OP.add)
        w = add("v", [lambda par=par: V.wait_ge(T.sem[par], (n - 1) * ne)], [], [A(rv)], 0.0, kind="w")
        ops[w]["deps"][p_in] = False
        for acc, ds in (("BA", (1, 2, 3, 4)), ("BB", (-1, -2, -3, -4))):
            cp(A(acc), A(ps))
            for d in ds:
                lo, hi = max(0, -d), min(5, 5 - d)
                o = 16 * ((rank + d) % n)
                tt(A(acc, 3 * lo, 3 * hi), A(acc, 3 * lo, 3 * hi), A(rv, o + 3 * (lo + d), o + 3 * (hi + d)), OP.min)
        tt(A("BC"), A("BA"), A("BB"), OP.min)
        cp(A("BI"), A("BC"))
        ts(A("UW"), A("BI"), 4095, OP.bitwise_and)
        ts(A("END"), A("BI"), 15, OP.arith_shift_right)
        ts(A("U16"), A("UW"), -2048.0, OP.add)
        tt(A("W1"), A("BC"), A(ps), OP.is_equal)
        ts(A("NBD"), A("BC"), BIG, OP.is_lt)
        tt(A("WON"), A("W1"), A("NBD"), OP.mult)
        tt(A("L1"), A("NBD"), A("WON"), OP.subtract)
        tt(A("LE"), A("END"), A("L1"), OP.mult)
        for s in range(1, 6):
            ts(A("CN6", 16 * s - 16, 16 * s), A("LE"), float(s), OP.is_ge)
        cp(A("CN6", 80, 96), A("WON"))
        tt(A("CW6"), A("CN6"), A("W6"), OP.mult)
        for x in range(8):
            if x < 4:
                ts(A("CM", x, 768, 8), A("CW6"), A("gm", x, x + 1), OP.mult)
            else:
                act(A("CM", x, 768, 8), A("CW6"), AF.Copy, scale=A("gm", x, x + 1))
        ts(A("NC6"), A("CN6"), -1.0, OP.mult, 1.0, OP.add)
        tt(A("ND6"), A("NC6"), A("D6"), OP.mult)
        tt(A("VP"), A("ND6"), A("WF"), OP.max)
        group([(A("ZR1", 0, 240), A("ones", 0, 128, p=1), A("C2K", p=1))] +
              [(A("ZR1", r, 240, 16), A("LR", 128 * r, 128 * r + 128), A("U16", 0, 15)) for r in range(16)])

        def lowest(es, bl, ex):
            for i, e in enumerate(es):
                for b in range(NB):
                    group([(A("ZR0", 16 * i + b, 16 * i + 16, 2, p=LN[b]),
                            A("EQ", e * 3600 + 240 * q + 128 * b, e * 3600 + 240 * q + 128 * b + LN[b]),
                            A("CM", (16 * e + q) * 8, (16 * e + q) * 8 + 8)) for q in range((8, 15)[b])])
            k = len(es)
            for b in range(NB):
                ts(A(bl, b, 16 * k, 2, p=LN[b]), A("ZR0", b, 16 * k, 2, p=LN[b]), A("thr", b, b + 1, p=LN[b]), OP.is_ge)
            tt(A(ex, 0, 128 * k), IND(bl, 0, 16 * k, "CE2", 0, 8 * k), A("MK", 0, 128 * k), OP.mult, ind=True)
            for i, e in enumerate(es):
                group([(A("ZR0", 512 + 16 * i, 528 + 16 * i), A("LG", 128 * x, 128 * x + 128),
                        A(ex, 128 * i + 16 * x, 128 * i + 16 * x + 16)) for x in range(8)])
            c, m = 16 * es[0], 16 * es[0] + 16 * k
            tt(A("OT", c, m), A("ZR0", 512, 512 + 16 * k), A("D6", c, m), OP.mult, two=False)
            tt(A("OT2", c, m), A("OT", c, m), A("VP", c, m), OP.max)
            cp(A("OFF", c, m), A("OT2", c, m))

        def change(e):
            up = "UP%d" % (e % 2)
            tt(A(up), A("OH", 240 * e, 240 * e + 240), A("ZR1", 0, 240), OP.mult, two=False)
            lw = IND("Kt", 0, 4096, wo, 16 * e, 16 * e + 15)
            tt(A("T1"), lw, A(up), OP.mult, ind=True)
            ts(A("T2"), A("T1"), 5, OP.arith_shift_right)
            if KS_PE:
                tt(A("KSF"), lw, A("OHS", 240 * e, 240 * e + 240), OP.add, ind=True)
                ps_ = A("MA", 0, 240)
                add("t", [lambda: PE.matmul(ps_[0], A("IDF")[0], A("KSF")[0], True, True)], [A("IDF"), A("KSF")], [ps_], 0.4)
                tt(A("T3"), A("T2"), ps_, OP.add, two=False)
            else:
                tt(A("KS"), lw, A("OHS", 240 * e, 240 * e + 240), OP.add, ind=True)
                tt(A("T3"), A("T2"), A("KS"), OP.add)
            ts(A("T4"), A("T3"), 4095, OP.bitwise_and)
            o = IND("Kt", 0, 4352, "OFF", 16 * e, 16 * e + 15)
            a = A("T4")
            add("v", [lambda: V.tensor_copy(o[0], a[0])], [a, (None, [o[1][1]], 0)], [(None, [o[1][0]], 0)], vcost(a, 1.0, True, True))
        lowest((4,), "BLW", "EXW")
        lowest((2, 3), "BL", "EXB")
        change(4)
        lowest((0, 1), "BL", "EXB")
        change(3)
        lowest((5,), "BLW", "EXW")
        change(2)
        o = IND("Xt", 0, 4352, "OFF", 80, 95)
        a = A("NX")
        add("v", [lambda o=o, a=a: V.tensor_copy(o[0], a[0])], [a, (None, [o[1][1]], 0)], [(None, [o[1][0]], 0)], vcost(a, 1.0, True, True))
        change(1)
        change(0)
        if t == 0:
            add("v", [lambda: V.tensor_reduce(A("WR")[0], A("WON")[0], AxisListType.X, OP.add)], [A("WON")], [A("WR")], 0.11)
            cp(A("WRB"), A("WR"))
            mm([(A("MA", 300, 301), A("ones", 0, 128), A("WRB"), True, True)])
            cp(A("WI"), A("MA", 300, 301))
            ts(A("WI2"), A("WI"), 1, OP.bitwise_and)
            ts(A("THR1"), A("WI2"), 2.0, OP.mult, T0, OP.add)
    group([(A("MA"), A("CI", 128 * a, 128 * a + 128), A("Xt", 512 * a, 512 * a + 512)) for a in range(8)])
    act(A("YX"), A("MA"), AF.Copy)
    dma("s", "ox", T.yx[:], T.YX[:], [A("YX")], [], 2.0)
    for a in range(8):
        ts(A("KF", 512 * a, 512 * a + 512), A("Kt", 512 * a, 512 * a + 512), -2048.0, OP.add)
    for a in range(8):
        mm([(A("MB"), A("CI", 128 * a, 128 * a + 128), A("KF", 512 * a, 512 * a + 512), a == 0, a == 7)])
    ts(A("YK"), A("MB"), 36.0 * 2048.0, OP.add)
    dma("y", "ok", T.yk[:], T.YK[:], [A("YK")], [], 2.0)
    return ops, ne


def order(ops):
    k = len(ops)
    succ = [[] for _ in range(k)]
    for i, o in enumerate(ops):
        for d in o["deps"]:
            succ[d].append(i)
    lat = 0.07
    prio = [0.0] * k
    for i in range(k - 1, -1, -1):
        prio[i] = ops[i]["cost"] + max([prio[j] + lat for j in succ[i]] or [0.0])
    rank = [prio[i] - ALPHA * i for i in range(k)]
    left = [len(o["deps"]) for o in ops]
    at = [0.0] * k
    free = {}
    pool = {}
    for i in range(k):
        if not left[i]:
            pool.setdefault(ops[i]["q"], []).append(i)
    done = []
    for _ in range(k):
        best = None
        for q, c in pool.items():
            if not c:
                continue
            f = free.get(q, 0.0)
            st = max(f, min(at[i] for i in c))
            i = max((i for i in c if at[i] <= st + 1e-9), key=lambda i: rank[i])
            if best is None or st < best[0]:
                best = (st, q, i)
        st, q, i = best
        pool[q].remove(i)
        o = ops[i]
        free[q] = st + (0.1 if o["kind"] == "d" else 0.0 if o["kind"] == "n" else o["cost"])
        end = st + o["cost"]
        done.append(i)
        for j in succ[i]:
            at[j] = max(at[j], end + (lat if o["kind"] != "w" and (ops[j]["deps"][i] or o["kind"] != "c") else 0.0))
            left[j] -= 1
            if not left[j]:
                pool.setdefault(ops[j]["q"], []).append(j)
    return done


def emit(g, T, ops, seq, ne):
    eng = {"v": g.vector, "s": g.scalar, "t": g.tensor, "g": g, "y": g.sync}
    count = {q: 0 for q in QS}
    known = {q: {} for q in eng}
    clock = {}
    sig = {}
    for i in seq:
        o = ops[i]
        q = o["q"]
        if o["kind"] == "n":
            continue
        need = {}
        for d, must in o["deps"].items():
            if must and d in sig:
                sem, val = sig[d]
                if known[q].get(sem, 0) < val:
                    need[sem] = max(need.get(sem, 0), val)
        for sem in sorted(need, key=lambda x: -len(clock[(x, need[x])])):
            if known[q].get(sem, 0) >= need[sem]:
                continue
            eng[q].wait_ge(T.sem[sem], need[sem])
            known[q][sem] = need[sem]
            for s2, v2 in clock[(sem, need[sem])].items():
                if known[q].get(s2, 0) < v2:
                    known[q][s2] = v2
        for c in o["calls"][:-1]:
            c()
        last = o["calls"][-1]()
        if o["kind"] == "c":
            count[q] += 1
            sem = "q" + q
            last.then_inc(T.sem[sem], 1)
            sig[i] = (sem, count[q])
            clock[(sem, count[q])] = dict(known[q])
        elif o["kind"] in ("d", "r"):
            sig[i] = o["sig"]
            clock[o["sig"]] = dict(known[q])
    for q in QS:
        if count[q]:
            g.wait_ge(T.sem["q" + q], count[q])
    for s in DMAS:
        g.wait_ge(T.sem[s], 16)
    g.wait_ge(T.sem["sent"], 3 * ne)


def rank_program(g, core, T, topo):
    if T.rank_of(core) is None:
        return
    ops, ne = build(g, core, T, topo)
    emit(g, T, ops, order(ops), ne)
